import numpy as np
import ml_dtypes


def mxq(x, axis, fmt="e4m3"):
    dtype, down = {"e4m3": (ml_dtypes.float8_e4m3fn, 7), "e5m2": (ml_dtypes.float8_e5m2, 14)}[fmt]
    v = np.moveaxis(np.asarray(x, np.float32).astype(ml_dtypes.bfloat16).astype(np.float64), axis, -1)
    blocks = v.reshape(v.shape[:-1] + (-1, 32))
    amax = np.abs(blocks).max(-1, keepdims=True)
    byte = np.maximum(np.where(amax > 0, np.frexp(amax)[1] - 1 + 127, 0) - down, 1)
    scale = np.exp2(byte - 127.0)
    codes = (blocks / scale).astype(np.float32).astype(dtype).astype(np.float64)
    return np.moveaxis((codes * scale).reshape(v.shape), -1, axis)


WIDE = False


def mx_kscale(k):
    if not WIDE:
        return np.ones(k)
    levels = np.array([10, -10, 5, -5, 0])
    if k % 512:
        return np.exp2(np.random.permutation(np.resize(levels, k // 32))).repeat(32)
    a = np.empty((k // 512, 16))
    for p in range(k // 512):
        a[p, :8] = np.random.permutation(np.resize(levels, 8))
        for g in range(8):
            far = levels[np.abs(levels - a[p, g]) >= 10]
            a[p, g + 8] = far[np.random.randint(len(far))]
    return np.exp2(a.ravel()).repeat(32)


def f64(x):
    return np.asarray(x).astype(np.float64)


def striped(idx):
    return np.tile(np.asarray(idx).reshape(-1, 16).T, (8, 1)).astype(np.uint16)


def unstriped(offs):
    return offs[:16].T.reshape(-1).astype(np.int64)


E2M1 = np.array([0.0, 0.5, 1.0, 1.5, 2.0, 3.0, 4.0, 6.0, -0.0, -0.5, -1.0, -1.5, -2.0, -3.0, -4.0, -6.0])


def pack_weight(w, fmt):
    k, n = w.shape
    w = f64(np.asarray(w, np.float32).astype(ml_dtypes.bfloat16)).reshape(k // 32, 32, n)
    amax = np.abs(w).max(1)
    if fmt == "e4m3":
        byte = np.frexp(amax)[1] - 1 + 127 - 7
    else:
        mant, ex = np.frexp(amax / 6.0)
        byte = np.where(mant > 0.5, ex, ex - 1) + 127
    byte = np.clip(np.where(amax > 0, byte, 1), 1, 254)
    scaled = (w * np.exp2(127.0 - byte)[:, None, :]).reshape(k, n).astype(np.float32)
    by_word = np.ascontiguousarray(scaled.reshape(k // 512, 128, 4, n).transpose(0, 1, 3, 2))
    if fmt == "e4m3":
        words = by_word.astype(ml_dtypes.float8_e4m3fn).view(np.uint8)
    else:
        c = by_word.astype(ml_dtypes.float4_e2m1fn).view(np.uint8) & 0xF
        words = (c[..., 0::2] | (c[..., 1::2] << 4)).reshape(k // 512, 128, 2 * n)
    return np.ascontiguousarray(words), np.ascontiguousarray(byte.astype(np.uint8).reshape(k // 512, 16, n))


def unpack_weight(words, scales, fmt):
    g, _, n = scales.shape
    words = np.ascontiguousarray(words).reshape(g, 128, n, -1)
    if fmt == "e4m3":
        vals = words.view(ml_dtypes.float8_e4m3fn).astype(np.float64)
    else:
        nib = np.empty((g, 128, n, 4), np.uint8)
        nib[..., 0::2] = words & 0xF
        nib[..., 1::2] = words >> 4
        vals = E2M1[nib]
    vals = vals * np.repeat(np.exp2(scales.astype(np.float64) - 127.0), 8, axis=1)[..., None]
    return vals.transpose(0, 1, 3, 2).reshape(g * 512, n)


B, N, T, D, NQ = 1, 512, 2048, 1024, 512
SEG = 16


def setup_inputs():
    n = np.random.standard_normal
    idx = np.random.permutation(T)[:B * N]
    s = mx_kscale(D)[:, None]
    kp = pack_weight(n((D, T)) / s, "e2m1")
    return {
        "qT": (n((B, D, NQ)) * s * (1.00 / np.sqrt(D))).astype(np.float32),
        "k_words": np.ascontiguousarray(kp[0].reshape(1, 2, 128, T, 2).transpose(0, 2, 3, 1, 4)).reshape(1, 128, T, 4),
        "k_scales": kp[1],
        "ts": np.tile(np.random.uniform(0.5, 2.0, 2048), (128, 1)).astype(np.float32),
        "hw": (np.random.uniform(-0.5, 1.0, (B, 1, NQ))).astype(np.float32),
        "offs": striped(idx),
    }


def reference(qT, k_words, k_scales, ts, hw, offs):
    idx = unstriped(offs)
    pick = lambda x, which: x[:, which].reshape(x.shape[0], B, -1).transpose(1, 0, 2)
    k = unpack_weight(k_words.reshape(1, 128, T, 2, 2).transpose(0, 3, 1, 2, 4).reshape(2, 128, 2 * T), k_scales, "e2m1")
    kg = pick(k, idx)
    qq = mxq(f64(qT), 1, "e4m3")
    a = kg.transpose(0, 2, 1) @ qq
    y = (np.maximum(a, 0.0) * f64(hw)).reshape(B, N, NQ // SEG, SEG).sum(-1) * pick(f64(ts), idx)[:, :1, :].transpose(0, 2, 1)
    return y

@@ -1,0 +1,175 @@
+from contextlib import ExitStack
+
+import concourse.mybir as mybir
+from concourse.masks import make_identity
+
+F32 = mybir.dt.float32
+BF16 = mybir.dt.bfloat16
+I32 = mybir.dt.int32
+U32 = mybir.dt.uint32
+U16 = mybir.dt.uint16
+U8 = mybir.dt.uint8
+FP8X4 = mybir.dt.float8_e4m3fn_x4
+FP4X4 = mybir.dt.float4_e2m1fn_x4
+ALU = mybir.AluOpType
+AX = mybir.AxisListType
+
+P = 128
+PACK = 4
+PASSES = 2
+K_PASS = P * PACK
+SLOTS, TOKENS, D, NQ, HEADS = 512, 2048, 1024, 512, 16
+QC = 128
+CHUNKS = NQ // QC
+KB = SLOTS // P
+RUNS = QC // HEADS
+
+FLOPS = 2 * SLOTS * D * NQ
+
+
+def tile_attend_tok_idxts_topk_kernel(tc, qT, k_words, k_scales, ts, hw, offs, out):
+    nc = tc.nc
+    with ExitStack() as ctx:
+        keep = ctx.enter_context(tc.tile_pool(name="keep", bufs=1))
+        psum = ctx.enter_context(tc.psum_pool(name="psum", bufs=1))
+
+        offsets = keep.tile([P, SLOTS // 16], U16, name="offsets")
+        nc.sync.dma_start(offsets[:], offs)
+
+        scale_pool = keep.tile([P, TOKENS], U8, name="scale_pool", align_bytes=64)
+        nc.vector.memset(scale_pool[:].bitcast(I32), 0)
+        for r in range(4):
+            nc.scalar.dma_start(
+                scale_pool[r:P:16, :].bitcast(I32),
+                k_scales[:, r:16:4, :].rearrange("o q t -> q o t").bitcast(I32),
+            )
+
+        raw = [[keep.tile([P, PACK, QC], F32, name=f"raw{c}_{o}") for o in range(PASSES)] for c in range(CHUNKS)]
+
+        def load_q(c):
+            for o in range(PASSES):
+                rows = qT[0, o * K_PASS : (o + 1) * K_PASS, c * QC : (c + 1) * QC]
+                nc.sync.dma_start(raw[c][o][:], rows.rearrange("(p t) q -> p t q", t=PACK))
+
+        load_q(0)
+        word_pool = keep.tile([P, TOKENS], U32, name="word_pool", align_bytes=64)
+        nc.sync.dma_start(word_pool[:].bitcast(I32), k_words[0].rearrange("p t b -> p (t b)").bitcast(I32))
+        for c in range(1, CHUNKS):
+            load_q(c)
+
+        hw_rows = keep.tile([P, PACK], F32, name="hw_rows")
+        nc.scalar.dma_start(hw_rows[:], hw[0, 0, :].rearrange("(p c) -> p c", c=PACK))
+        identity = keep.tile([P, P], F32, name="identity")
+        make_identity(nc, identity[:])
+
+        ts_pool = keep.tile([P, TOKENS], F32, name="ts_pool")
+        nc.vector.memset(ts_pool[:], 0.0)
+        nc.scalar.dma_start(ts_pool[0:1, :], ts[0:1, :])
+
+        k_scale1 = keep.tile([P, SLOTS], U8, name="k_scale1", align_bytes=64)
+        nc.vector.memset(k_scale1[:].bitcast(I32), 0)
+
+        k_scale0 = keep.tile([P, SLOTS], U8, name="k_scale0", align_bytes=64)
+        nc.vector.tensor_copy(k_scale0[:], scale_pool[:].indirect(offsets[:]))
+        k_scale = [k_scale0, k_scale1]
+
+        grouped = [keep.tile([P, PASSES, QC, PACK], BF16, name=f"grouped{c}", align_bytes=64) for c in range(CHUNKS)]
+        q_codes = [keep.tile([P, PASSES, QC], U32, name=f"q_codes{c}", align_bytes=64) for c in range(CHUNKS)]
+        q_scale = [keep.tile([P, PASSES, QC], U8, name=f"q_scale{c}", align_bytes=64) for c in range(CHUNKS)]
+
+        def cast(c):
+            for o in range(PASSES):
+                nc.scalar.copy(
+                    grouped[c][:, o, :, :].rearrange("p (g i) t -> p g t i", i=4),
+                    raw[c][o][:].rearrange("p t (g i) -> p g t i", i=4),
+                )
+
+        def quantize(c):
+            nc.vector.quantize_mx(
+                out=q_codes[c][:].rearrange("p o q -> p (o q)").bitcast(FP8X4),
+                scales=q_scale[c][:].rearrange("p o q -> p (o q)"),
+                in_=grouped[c][:].rearrange("p o q t -> p (o q t)"),
+            )
+
+        cast(0)
+        nc.scalar.dma_start(k_scale1[0:112, :].bitcast(I32), k_scale0[16:128, :].bitcast(I32))
+
+        ts_listed = keep.tile([P, SLOTS], F32, name="ts_listed")
+        nc.vector.tensor_copy(ts_listed[:], ts_pool[:].indirect(offsets[:]))
+
+        hw_turned = psum.tile([P, PACK, P], F32, name="hw_turned")
+        for c in range(PACK):
+            nc.tensor.transpose(hw_turned[:, c, :], hw_rows[:, c : c + 1].to_broadcast([P, P]), identity[:])
+        ts_turned = psum.tile([P, KB, P], F32, name="ts_turned")
+        for b in range(KB):
+            nc.tensor.transpose(ts_turned[:, b, :], ts_listed[:, b * P : (b + 1) * P], identity[:])
+
+        quantize(0)
+        word_pairs = keep.tile([P, SLOTS], U32, name="word_pairs", align_bytes=64)
+        nc.vector.tensor_copy(word_pairs[:], word_pool[:].indirect(offsets[:]))
+        k_codes = keep.tile([P, PASSES, SLOTS], U16, name="k_codes", align_bytes=64)
+        nc.vector.tensor_copy(k_codes[:], word_pairs[:].bitcast(U16).rearrange("p (i o) -> p o i", o=PASSES))
+
+        cast(1)
+        hw_all = keep.tile([P, NQ], F32, name="hw_all")
+        nc.scalar.copy(hw_all[:].rearrange("m (p c) -> m p c", c=PACK), hw_turned[:].rearrange("m c p -> m p c"))
+
+        scores = [psum.tile([P, KB, QC], F32, name=f"scores{c}") for c in range(CHUNKS)]
+        weighted = [keep.tile([P, KB, QC], F32, name=f"weighted{c}") for c in range(CHUNKS)]
+        summed = keep.tile([P, KB, NQ // HEADS], F32, name="summed")
+
+        def multiply(c):
+            for b in range(KB):
+                keys = slice(b * P, (b + 1) * P)
+                for o in range(PASSES):
+                    nc.tensor.matmul_mx(
+                        out=scores[c][:, b, :],
+                        lhsT=k_codes[:, o, keys].bitcast(FP4X4),
+                        lhsT_scale=k_scale[o][:, keys],
+                        rhs=q_codes[c][:, o, :].bitcast(FP8X4),
+                        rhs_scale=q_scale[c][:, o, :],
+                        start=(o == 0),
+                        stop=(o == PASSES - 1),
+                    )
+
+        def weigh(c):
+            nc.vector.scalar_tensor_tensor(
+                out=weighted[c][:],
+                in0=scores[c][:],
+                scalar=0.0,
+                in1=hw_all[:, c * QC : (c + 1) * QC].unsqueeze(1).to_broadcast([P, KB, QC]),
+                op0=ALU.max,
+                op1=ALU.mult,
+            )
+
+        def add_heads(c):
+            nc.vector.tensor_reduce(
+                out=summed[:, :, c * RUNS : (c + 1) * RUNS],
+                in_=weighted[c][:].rearrange("p b (j s) -> p b j s", s=HEADS),
+                axis=AX.X,
+                op=ALU.add,
+            )
+
+        multiply(0)
+        quantize(1)
+        multiply(1)
+        cast(2)
+        cast(3)
+        weigh(0)
+        quantize(2)
+        multiply(2)
+        add_heads(0)
+        weigh(1)
+        quantize(3)
+        multiply(3)
+        add_heads(1)
+        weigh(2)
+        weigh(3)
+        add_heads(2)
+        add_heads(3)
+
+        result = keep.tile([P, KB, NQ // HEADS], F32, name="result")
+        nc.vector.tensor_tensor(
+            result[:], summed[:], ts_turned[:, :, 0:1].to_broadcast([P, KB, NQ // HEADS]), ALU.mult
+        )
+        nc.sync.dma_start(out[0].rearrange("(b p) j -> p b j", p=P), result[:])

@@ -1,7 +1,6 @@
 from contextlib import ExitStack
 
 import concourse.mybir as mybir
-from concourse.masks import make_identity
 
 F32 = mybir.dt.float32
 BF16 = mybir.dt.bfloat16
@@ -31,94 +30,102 @@ def tile_attend_tok_idxts_topk_kernel(tc, qT, k_words, k_scales, ts, hw, offs, o
     nc = tc.nc
     with ExitStack() as ctx:
         keep = ctx.enter_context(tc.tile_pool(name="keep", bufs=1))
+        ring = ctx.enter_context(tc.tile_pool(name="ring", bufs=2))
         psum = ctx.enter_context(tc.psum_pool(name="psum", bufs=1))
+        banks = ctx.enter_context(tc.psum_pool(name="banks", bufs=CHUNKS))
 
         offsets = keep.tile([P, SLOTS // 16], U16, name="offsets")
         nc.sync.dma_start(offsets[:], offs)
+        hw_rows = keep.tile([P, PACK], F32, name="hw_rows")
+        nc.scalar.dma_start(hw_rows[:], hw[0, 0, :].rearrange("(p c) -> p c", c=PACK))
+        ts_row = keep.tile([1, TOKENS], F32, name="ts_row")
+        nc.scalar.dma_start(ts_row[:], ts[0:1, :])
 
         scale_pool = keep.tile([P, TOKENS], U8, name="scale_pool", align_bytes=64)
         nc.vector.memset(scale_pool[:].bitcast(I32), 0)
         for r in range(4):
-            nc.scalar.dma_start(
+            nc.sync.dma_start(
                 scale_pool[r:P:16, :].bitcast(I32),
                 k_scales[:, r:16:4, :].rearrange("o q t -> q o t").bitcast(I32),
             )
 
-        raw = [[keep.tile([P, PACK, QC], F32, name=f"raw{c}_{o}") for o in range(PASSES)] for c in range(CHUNKS)]
-
-        def load_q(c):
-            for o in range(PASSES):
-                rows = qT[0, o * K_PASS : (o + 1) * K_PASS, c * QC : (c + 1) * QC]
-                nc.sync.dma_start(raw[c][o][:], rows.rearrange("(p t) q -> p t q", t=PACK))
-
-        load_q(0)
-        word_pool = keep.tile([P, TOKENS], U32, name="word_pool", align_bytes=64)
-        nc.sync.dma_start(word_pool[:].bitcast(I32), k_words[0].rearrange("p t b -> p (t b)").bitcast(I32))
-        for c in range(1, CHUNKS):
-            load_q(c)
-
-        hw_rows = keep.tile([P, PACK], F32, name="hw_rows")
-        nc.scalar.dma_start(hw_rows[:], hw[0, 0, :].rearrange("(p c) -> p c", c=PACK))
         identity = keep.tile([P, P], F32, name="identity")
-        make_identity(nc, identity[:])
+        with tc.tile_pool(name="setup", bufs=1) as setup:
+            zeros = setup.tile([P, P], F32, name="zeros")
+            nc.vector.memset(zeros[:], 0.0)
+            nc.gpsimd.affine_select(
+                out=identity[:],
+                in_=zeros[:],
+                compare_op=ALU.not_equal,
+                fill=1.0,
+                base=0,
+                pattern=[[-1, P]],
+                channel_multiplier=1,
+            )
+        loads = ctx.enter_context(tc.tile_pool(name="loads", bufs=1))
 
-        ts_pool = keep.tile([P, TOKENS], F32, name="ts_pool")
-        nc.vector.memset(ts_pool[:], 0.0)
-        nc.scalar.dma_start(ts_pool[0:1, :], ts[0:1, :])
+        word_pool = loads.tile([P, TOKENS], U32, name="word_pool", align_bytes=64)
+        nc.sync.dma_start(word_pool[:].bitcast(I32), k_words[0].rearrange("p t b -> p (t b)").bitcast(I32))
+
+        raw = {}
+
+        def load_q(o, c, n):
+            tile = loads.tile([P, PACK, n * QC], F32, name=f"raw{o}_{c}")
+            rows = qT[0, o * K_PASS : (o + 1) * K_PASS, c * QC : (c + n) * QC]
+            nc.sync.dma_start(tile[:], rows.rearrange("(p t) q -> p t q", t=PACK))
+            for k in range(n):
+                raw[o, c + k] = tile[:, :, k * QC : (k + 1) * QC]
+
+        for c in range(0, CHUNKS, 2):
+            load_q(0, c, 2)
+            load_q(1, c, 1)
+            load_q(1, c + 1, 1)
 
         k_scale1 = keep.tile([P, SLOTS], U8, name="k_scale1", align_bytes=64)
         nc.vector.memset(k_scale1[:].bitcast(I32), 0)
+        ts_pool = keep.tile([P, TOKENS], F32, name="ts_pool")
+        nc.vector.memset(ts_pool[:].bitcast(I32), 0)
+        nc.vector.tensor_copy(ts_pool[0:1, :], ts_row[:])
 
         k_scale0 = keep.tile([P, SLOTS], U8, name="k_scale0", align_bytes=64)
         nc.vector.tensor_copy(k_scale0[:], scale_pool[:].indirect(offsets[:]))
-        k_scale = [k_scale0, k_scale1]
-
-        grouped = [keep.tile([P, PASSES, QC, PACK], BF16, name=f"grouped{c}", align_bytes=64) for c in range(CHUNKS)]
-        q_codes = [keep.tile([P, PASSES, QC], U32, name=f"q_codes{c}", align_bytes=64) for c in range(CHUNKS)]
-        q_scale = [keep.tile([P, PASSES, QC], U8, name=f"q_scale{c}", align_bytes=64) for c in range(CHUNKS)]
-
-        def cast(c):
-            for o in range(PASSES):
-                nc.scalar.copy(
-                    grouped[c][:, o, :, :].rearrange("p (g i) t -> p g t i", i=4),
-                    raw[c][o][:].rearrange("p t (g i) -> p g t i", i=4),
-                )
-
-        def quantize(c):
-            nc.vector.quantize_mx(
-                out=q_codes[c][:].rearrange("p o q -> p (o q)").bitcast(FP8X4),
-                scales=q_scale[c][:].rearrange("p o q -> p (o q)"),
-                in_=grouped[c][:].rearrange("p o q t -> p (o q t)"),
-            )
-
-        cast(0)
         nc.scalar.dma_start(k_scale1[0:112, :].bitcast(I32), k_scale0[16:128, :].bitcast(I32))
-
-        ts_listed = keep.tile([P, SLOTS], F32, name="ts_listed")
-        nc.vector.tensor_copy(ts_listed[:], ts_pool[:].indirect(offsets[:]))
+        k_scale = [k_scale0, k_scale1]
 
         hw_turned = psum.tile([P, PACK, P], F32, name="hw_turned")
         for c in range(PACK):
             nc.tensor.transpose(hw_turned[:, c, :], hw_rows[:, c : c + 1].to_broadcast([P, P]), identity[:])
-        ts_turned = psum.tile([P, KB, P], F32, name="ts_turned")
-        for b in range(KB):
-            nc.tensor.transpose(ts_turned[:, b, :], ts_listed[:, b * P : (b + 1) * P], identity[:])
+        hw_all = keep.tile([P, NQ], F32, name="hw_all")
+        nc.scalar.copy(hw_all[:].rearrange("m (p c) -> m p c", c=PACK), hw_turned[:].rearrange("m c p -> m p c"))
 
-        quantize(0)
+        ts_listed = keep.tile([P, SLOTS], F32, name="ts_listed")
+        nc.vector.tensor_copy(ts_listed[:], ts_pool[:].indirect(offsets[:]))
+
         word_pairs = keep.tile([P, SLOTS], U32, name="word_pairs", align_bytes=64)
         nc.vector.tensor_copy(word_pairs[:], word_pool[:].indirect(offsets[:]))
         k_codes = keep.tile([P, PASSES, SLOTS], U16, name="k_codes", align_bytes=64)
         nc.vector.tensor_copy(k_codes[:], word_pairs[:].bitcast(U16).rearrange("p (i o) -> p o i", o=PASSES))
 
-        cast(1)
-        hw_all = keep.tile([P, NQ], F32, name="hw_all")
-        nc.scalar.copy(hw_all[:].rearrange("m (p c) -> m p c", c=PACK), hw_turned[:].rearrange("m c p -> m p c"))
-
-        scores = [psum.tile([P, KB, QC], F32, name=f"scores{c}") for c in range(CHUNKS)]
+        grouped = [keep.tile([P, PASSES, QC, PACK], BF16, name=f"grouped{c}", align_bytes=64) for c in range(CHUNKS)]
         weighted = [keep.tile([P, KB, QC], F32, name=f"weighted{c}") for c in range(CHUNKS)]
         summed = keep.tile([P, KB, NQ // HEADS], F32, name="summed")
+        scores = {}
 
-        def multiply(c):
+        def cast(o, c):
+            nc.scalar.copy(
+                grouped[c][:, o, :, :].rearrange("p (g i) t -> p g t i", i=4),
+                raw[o, c].rearrange("p t (g i) -> p g t i", i=4),
+            )
+
+        def score(c):
+            q_codes = ring.tile([P, PASSES, QC], U32, name="q_codes", align_bytes=64)
+            q_scale = ring.tile([P, PASSES, QC], U8, name="q_scale", align_bytes=64)
+            nc.vector.quantize_mx(
+                out=q_codes[:].rearrange("p o q -> p (o q)").bitcast(FP8X4),
+                scales=q_scale[:].rearrange("p o q -> p (o q)"),
+                in_=grouped[c][:].rearrange("p o q t -> p (o q t)"),
+            )
+            scores[c] = banks.tile([P, KB, QC], F32, name="bank")
             for b in range(KB):
                 keys = slice(b * P, (b + 1) * P)
                 for o in range(PASSES):
@@ -126,8 +133,8 @@ def tile_attend_tok_idxts_topk_kernel(tc, qT, k_words, k_scales, ts, hw, offs, o
                         out=scores[c][:, b, :],
                         lhsT=k_codes[:, o, keys].bitcast(FP4X4),
                         lhsT_scale=k_scale[o][:, keys],
-                        rhs=q_codes[c][:, o, :].bitcast(FP8X4),
-                        rhs_scale=q_scale[c][:, o, :],
+                        rhs=q_codes[:, o, :].bitcast(FP8X4),
+                        rhs_scale=q_scale[:, o, :],
                         start=(o == 0),
                         stop=(o == PASSES - 1),
                     )
@@ -150,18 +157,18 @@ def tile_attend_tok_idxts_topk_kernel(tc, qT, k_words, k_scales, ts, hw, offs, o
                 op=ALU.add,
             )
 
-        multiply(0)
-        quantize(1)
-        multiply(1)
-        cast(2)
-        cast(3)
+        for o, c in [(0, 0), (1, 0), (0, 1), (1, 1), (0, 2), (0, 3), (1, 2), (1, 3)]:
+            cast(o, c)
+        score(0)
+        score(1)
         weigh(0)
-        quantize(2)
-        multiply(2)
         add_heads(0)
+        score(2)
         weigh(1)
-        quantize(3)
-        multiply(3)
+        score(3)
+        ts_turned = banks.tile([P, KB, P], F32, name="bank")
+        for b in range(KB):
+            nc.tensor.transpose(ts_turned[:, b, :], ts_listed[:, b * P : (b + 1) * P], identity[:])
         add_heads(1)
         weigh(2)
         weigh(3)

@@ -32,14 +32,11 @@ def tile_attend_tok_idxts_topk_kernel(tc, qT, k_words, k_scales, ts, hw, offs, o
         keep = ctx.enter_context(tc.tile_pool(name="keep", bufs=1))
         ring = ctx.enter_context(tc.tile_pool(name="ring", bufs=2))
         psum = ctx.enter_context(tc.psum_pool(name="psum", bufs=1))
-        banks = ctx.enter_context(tc.psum_pool(name="banks", bufs=CHUNKS))
 
         offsets = keep.tile([P, SLOTS // 16], U16, name="offsets")
         nc.sync.dma_start(offsets[:], offs)
         hw_rows = keep.tile([P, PACK], F32, name="hw_rows")
         nc.scalar.dma_start(hw_rows[:], hw[0, 0, :].rearrange("(p c) -> p c", c=PACK))
-        ts_row = keep.tile([1, TOKENS], F32, name="ts_row")
-        nc.scalar.dma_start(ts_row[:], ts[0:1, :])
 
         scale_pool = keep.tile([P, TOKENS], U8, name="scale_pool", align_bytes=64)
         nc.vector.memset(scale_pool[:].bitcast(I32), 0)
@@ -76,20 +73,19 @@ def tile_attend_tok_idxts_topk_kernel(tc, qT, k_words, k_scales, ts, hw, offs, o
             for k in range(n):
                 raw[o, c + k] = tile[:, :, k * QC : (k + 1) * QC]
 
-        for c in range(0, CHUNKS, 2):
-            load_q(0, c, 2)
-            load_q(1, c, 1)
-            load_q(1, c + 1, 1)
+        for c in range(CHUNKS):
+            for o in range(PASSES):
+                load_q(o, c, 1)
 
         k_scale1 = keep.tile([P, SLOTS], U8, name="k_scale1", align_bytes=64)
         nc.vector.memset(k_scale1[:].bitcast(I32), 0)
         ts_pool = keep.tile([P, TOKENS], F32, name="ts_pool")
         nc.vector.memset(ts_pool[:].bitcast(I32), 0)
-        nc.vector.tensor_copy(ts_pool[0:1, :], ts_row[:])
+        nc.gpsimd.dma_start(ts_pool[0:1, :], ts[0:1, :])
 
         k_scale0 = keep.tile([P, SLOTS], U8, name="k_scale0", align_bytes=64)
         nc.vector.tensor_copy(k_scale0[:], scale_pool[:].indirect(offsets[:]))
-        nc.scalar.dma_start(k_scale1[0:112, :].bitcast(I32), k_scale0[16:128, :].bitcast(I32))
+        nc.gpsimd.dma_start(k_scale1[0:112, :].bitcast(I32), k_scale0[16:128, :].bitcast(I32))
         k_scale = [k_scale0, k_scale1]
 
         hw_turned = psum.tile([P, PACK, P], F32, name="hw_turned")
@@ -98,15 +94,12 @@ def tile_attend_tok_idxts_topk_kernel(tc, qT, k_words, k_scales, ts, hw, offs, o
         hw_all = keep.tile([P, NQ], F32, name="hw_all")
         nc.scalar.copy(hw_all[:].rearrange("m (p c) -> m p c", c=PACK), hw_turned[:].rearrange("m c p -> m p c"))
 
-        ts_listed = keep.tile([P, SLOTS], F32, name="ts_listed")
-        nc.vector.tensor_copy(ts_listed[:], ts_pool[:].indirect(offsets[:]))
-
         word_pairs = keep.tile([P, SLOTS], U32, name="word_pairs", align_bytes=64)
         nc.vector.tensor_copy(word_pairs[:], word_pool[:].indirect(offsets[:]))
         k_codes = keep.tile([P, PASSES, SLOTS], U16, name="k_codes", align_bytes=64)
         nc.vector.tensor_copy(k_codes[:], word_pairs[:].bitcast(U16).rearrange("p (i o) -> p o i", o=PASSES))
 
-        grouped = [keep.tile([P, PASSES, QC, PACK], BF16, name=f"grouped{c}", align_bytes=64) for c in range(CHUNKS)]
+        grouped = [keep.tile([P, PASSES, QC, PACK], BF16, name=f"grouped{c}", tag=f"grouped{c}", align_bytes=64) for c in range(CHUNKS)]
         weighted = [keep.tile([P, KB, QC], F32, name=f"weighted{c}") for c in range(CHUNKS)]
         summed = keep.tile([P, KB, NQ // HEADS], F32, name="summed")
         scores = {}
@@ -125,7 +118,7 @@ def tile_attend_tok_idxts_topk_kernel(tc, qT, k_words, k_scales, ts, hw, offs, o
                 scales=q_scale[:].rearrange("p o q -> p (o q)"),
                 in_=grouped[c][:].rearrange("p o q t -> p (o q t)"),
             )
-            scores[c] = banks.tile([P, KB, QC], F32, name="bank")
+            scores[c] = psum.tile([P, KB, QC], F32, name=f"bank{c}")
             for b in range(KB):
                 keys = slice(b * P, (b + 1) * P)
                 for o in range(PASSES):
@@ -157,20 +150,23 @@ def tile_attend_tok_idxts_topk_kernel(tc, qT, k_words, k_scales, ts, hw, offs, o
                 op=ALU.add,
             )
 
-        for o, c in [(0, 0), (1, 0), (0, 1), (1, 1), (0, 2), (0, 3), (1, 2), (1, 3)]:
-            cast(o, c)
+        for c in range(CHUNKS):
+            for o in range(PASSES):
+                cast(o, c)
         score(0)
+        ts_listed = keep.tile([P, SLOTS], F32, name="ts_listed", tag="grouped0", align_bytes=64)
+        nc.vector.tensor_copy(ts_listed[:], ts_pool[:].indirect(offsets[:]))
         score(1)
         weigh(0)
         add_heads(0)
         score(2)
         weigh(1)
         score(3)
-        ts_turned = banks.tile([P, KB, P], F32, name="bank")
-        for b in range(KB):
-            nc.tensor.transpose(ts_turned[:, b, :], ts_listed[:, b * P : (b + 1) * P], identity[:])
         add_heads(1)
         weigh(2)
+        ts_turned = psum.tile([P, KB, P], F32, name="bank2")
+        for b in range(KB):
+            nc.tensor.transpose(ts_turned[:, b, :], ts_listed[:, b * P : (b + 1) * P], identity[:])
         weigh(3)
         add_heads(2)
         add_heads(3)

@@ -38,11 +38,11 @@ def tile_attend_tok_idxts_topk_kernel(tc, qT, k_words, k_scales, ts, hw, offs, o
         hw_rows = keep.tile([P, PACK], F32, name="hw_rows")
         nc.scalar.dma_start(hw_rows[:], hw[0, 0, :].rearrange("(p c) -> p c", c=PACK))
 
-        scale_pool = keep.tile([P, TOKENS], U8, name="scale_pool", align_bytes=64)
-        nc.vector.memset(scale_pool[:].bitcast(I32), 0)
+        scale_pool = keep.tile([P, PASSES, TOKENS], U8, name="scale_pool", align_bytes=64)
+        nc.vector.memset(scale_pool[:].rearrange("p o t -> p (o t)").bitcast(I32), 0)
         for r in range(4):
             nc.sync.dma_start(
-                scale_pool[r:P:16, :].bitcast(I32),
+                scale_pool[r:P:32, :, :].bitcast(I32),
                 k_scales[:, r:16:4, :].rearrange("o q t -> q o t").bitcast(I32),
             )
 
@@ -67,7 +67,7 @@ def tile_attend_tok_idxts_topk_kernel(tc, qT, k_words, k_scales, ts, hw, offs, o
         raw = {}
 
         def load_q(o, c, n):
-            tile = loads.tile([P, PACK, n * QC], F32, name=f"raw{o}_{c}")
+            tile = (keep if (o, c) == (0, 0) else loads).tile([P, PACK, n * QC], F32, name=f"raw{o}_{c}")
             rows = qT[0, o * K_PASS : (o + 1) * K_PASS, c * QC : (c + n) * QC]
             nc.sync.dma_start(tile[:], rows.rearrange("(p t) q -> p t q", t=PACK))
             for k in range(n):
@@ -77,16 +77,13 @@ def tile_attend_tok_idxts_topk_kernel(tc, qT, k_words, k_scales, ts, hw, offs, o
             for o in range(PASSES):
                 load_q(o, c, 1)
 
-        k_scale1 = keep.tile([P, SLOTS], U8, name="k_scale1", align_bytes=64)
-        nc.vector.memset(k_scale1[:].bitcast(I32), 0)
         ts_pool = keep.tile([P, TOKENS], F32, name="ts_pool")
         nc.vector.memset(ts_pool[:].bitcast(I32), 0)
-        nc.gpsimd.dma_start(ts_pool[0:1, :], ts[0:1, :])
+        nc.scalar.dma_start(ts_pool[0:1, :], ts[0:1, :])
 
-        k_scale0 = keep.tile([P, SLOTS], U8, name="k_scale0", align_bytes=64)
-        nc.vector.tensor_copy(k_scale0[:], scale_pool[:].indirect(offsets[:]))
-        nc.gpsimd.dma_start(k_scale1[0:112, :].bitcast(I32), k_scale0[16:128, :].bitcast(I32))
-        k_scale = [k_scale0, k_scale1]
+        k_scale = keep.tile([P, PASSES, SLOTS], U8, name="k_scale", align_bytes=64)
+        for o in range(PASSES):
+            nc.vector.tensor_copy(k_scale[:, o, :], scale_pool[:, o, :].indirect(offsets[:]))
 
         hw_turned = psum.tile([P, PACK, P], F32, name="hw_turned")
         for c in range(PACK):
@@ -100,7 +97,7 @@ def tile_attend_tok_idxts_topk_kernel(tc, qT, k_words, k_scales, ts, hw, offs, o
         nc.vector.tensor_copy(k_codes[:], word_pairs[:].bitcast(U16).rearrange("p (i o) -> p o i", o=PASSES))
 
         grouped = [keep.tile([P, PASSES, QC, PACK], BF16, name=f"grouped{c}", tag=f"grouped{c}", align_bytes=64) for c in range(CHUNKS)]
-        weighted = [keep.tile([P, KB, QC], F32, name=f"weighted{c}") for c in range(CHUNKS)]
+        weighted = {}
         summed = keep.tile([P, KB, NQ // HEADS], F32, name="summed")
         scores = {}
 
@@ -125,7 +122,7 @@ def tile_attend_tok_idxts_topk_kernel(tc, qT, k_words, k_scales, ts, hw, offs, o
                     nc.tensor.matmul_mx(
                         out=scores[c][:, b, :],
                         lhsT=k_codes[:, o, keys].bitcast(FP4X4),
-                        lhsT_scale=k_scale[o][:, keys],
+                        lhsT_scale=k_scale[:, o, keys],
                         rhs=q_codes[:, o, :].bitcast(FP8X4),
                         rhs_scale=q_scale[:, o, :],
                         start=(o == 0),
@@ -133,6 +130,7 @@ def tile_attend_tok_idxts_topk_kernel(tc, qT, k_words, k_scales, ts, hw, offs, o
                     )
 
         def weigh(c):
+            weighted[c] = keep.tile([P, KB, QC], F32, name="weighted", tag=f"grouped{c + 1}", align_bytes=64)
             nc.vector.scalar_tensor_tensor(
                 out=weighted[c][:],
                 in0=scores[c][:],
@@ -158,8 +156,8 @@ def tile_attend_tok_idxts_topk_kernel(tc, qT, k_words, k_scales, ts, hw, offs, o
         nc.vector.tensor_copy(ts_listed[:], ts_pool[:].indirect(offsets[:]))
         score(1)
         weigh(0)
-        add_heads(0)
         score(2)
+        add_heads(0)
         weigh(1)
         score(3)
         add_heads(1)

@@ -22,6 +22,8 @@ QC = 128
 CHUNKS = NQ // QC
 KB = SLOTS // P
 RUNS = QC // HEADS
+SHIFT = 16
+TS_ROW = 8
 
 FLOPS = 2 * SLOTS * D * NQ
 
@@ -35,55 +37,59 @@ def tile_attend_tok_idxts_topk_kernel(tc, qT, k_words, k_scales, ts, hw, offs, o
 
         offsets = keep.tile([P, SLOTS // 16], U16, name="offsets")
         nc.sync.dma_start(offsets[:], offs)
-        hw_rows = keep.tile([P, PACK], F32, name="hw_rows")
+        hw_rows = keep.tile([P, PACK], F32, name="hw_rows", tag="stage0", align_bytes=64)
         nc.scalar.dma_start(hw_rows[:], hw[0, 0, :].rearrange("(p c) -> p c", c=PACK))
-
-        scale_pool = keep.tile([P, PASSES, TOKENS], U8, name="scale_pool", align_bytes=64)
-        nc.vector.memset(scale_pool[:].rearrange("p o t -> p (o t)").bitcast(I32), 0)
-        for r in range(4):
-            nc.sync.dma_start(
-                scale_pool[r:P:32, :, :].bitcast(I32),
-                k_scales[:, r:16:4, :].rearrange("o q t -> q o t").bitcast(I32),
-            )
-
-        identity = keep.tile([P, P], F32, name="identity")
-        with tc.tile_pool(name="setup", bufs=1) as setup:
-            zeros = setup.tile([P, P], F32, name="zeros")
-            nc.vector.memset(zeros[:], 0.0)
-            nc.gpsimd.affine_select(
-                out=identity[:],
-                in_=zeros[:],
-                compare_op=ALU.not_equal,
-                fill=1.0,
-                base=0,
-                pattern=[[-1, P]],
-                channel_multiplier=1,
-            )
-        loads = ctx.enter_context(tc.tile_pool(name="loads", bufs=1))
-
-        word_pool = loads.tile([P, TOKENS], U32, name="word_pool", align_bytes=64)
-        nc.sync.dma_start(word_pool[:].bitcast(I32), k_words[0].rearrange("p t b -> p (t b)").bitcast(I32))
 
         raw = {}
 
         def load_q(o, c, n):
-            tile = (keep if (o, c) == (0, 0) else loads).tile([P, PACK, n * QC], F32, name=f"raw{o}_{c}")
+            tile = keep.tile([P, PACK, n * QC], F32, name=f"raw{o}_{c}")
             rows = qT[0, o * K_PASS : (o + 1) * K_PASS, c * QC : (c + n) * QC]
             nc.sync.dma_start(tile[:], rows.rearrange("(p t) q -> p t q", t=PACK))
             for k in range(n):
                 raw[o, c + k] = tile[:, :, k * QC : (k + 1) * QC]
 
-        for c in range(CHUNKS):
-            for o in range(PASSES):
-                load_q(o, c, 1)
+        word_pool = keep.tile([P, TOKENS], U32, name="word_pool", align_bytes=64)
+        words = k_words[0].rearrange("p t b -> p (t b)").bitcast(I32)
+        nc.sync.dma_start(word_pool[:, : TOKENS // 2].bitcast(I32), words[:, : TOKENS // 2])
+
+        scale_pool = keep.tile([P, TOKENS], U8, name="scale_pool", align_bytes=64)
+        nc.vector.memset(scale_pool[:].bitcast(I32), 0)
+        for r in range(4):
+            nc.sync.dma_start(
+                scale_pool[r:P:SHIFT, :].bitcast(I32),
+                k_scales[:, r:16:4, :].rearrange("o q t -> q o t").bitcast(I32),
+            )
+
+        nc.sync.dma_start(word_pool[:, TOKENS // 2 :].bitcast(I32), words[:, TOKENS // 2 :])
+        load_q(0, 0, 1)
+        load_q(1, 0, 1)
 
         ts_pool = keep.tile([P, TOKENS], F32, name="ts_pool")
         nc.vector.memset(ts_pool[:].bitcast(I32), 0)
-        nc.scalar.dma_start(ts_pool[0:1, :], ts[0:1, :])
+        nc.sync.dma_start(ts_pool[TS_ROW : TS_ROW + 1, :], ts[0:1, :])
 
-        k_scale = keep.tile([P, PASSES, SLOTS], U8, name="k_scale", align_bytes=64)
-        for o in range(PASSES):
-            nc.vector.tensor_copy(k_scale[:, o, :], scale_pool[:, o, :].indirect(offsets[:]))
+        load_q(0, 1, 1)
+        load_q(1, 1, 1)
+
+        k_scale = [keep.tile([P, SLOTS], U8, name=f"k_scale{o}", align_bytes=64) for o in range(PASSES)]
+        nc.vector.memset(k_scale[1][:].bitcast(I32), 0)
+        nc.vector.tensor_copy(k_scale[0][:], scale_pool[:].indirect(offsets[:]))
+        nc.sync.dma_start(k_scale[1][0 : P - SHIFT, :].bitcast(I32), k_scale[0][SHIFT:P, :].bitcast(I32))
+        load_q(0, 2, 2)
+        load_q(1, 2, 2)
+
+        identity = keep.tile([P, P], F32, name="identity")
+        nc.gpsimd.memset(identity[:], 0.0)
+        nc.gpsimd.affine_select(
+            out=identity[:],
+            in_=identity[:],
+            compare_op=ALU.not_equal,
+            fill=1.0,
+            base=0,
+            pattern=[[-1, P]],
+            channel_multiplier=1,
+        )
 
         hw_turned = psum.tile([P, PACK, P], F32, name="hw_turned")
         for c in range(PACK):
@@ -91,12 +97,15 @@ def tile_attend_tok_idxts_topk_kernel(tc, qT, k_words, k_scales, ts, hw, offs, o
         hw_all = keep.tile([P, NQ], F32, name="hw_all")
         nc.scalar.copy(hw_all[:].rearrange("m (p c) -> m p c", c=PACK), hw_turned[:].rearrange("m c p -> m p c"))
 
-        word_pairs = keep.tile([P, SLOTS], U32, name="word_pairs", align_bytes=64)
+        word_pairs = keep.tile([P, SLOTS], U32, name="word_pairs", tag="word_pairs", align_bytes=64)
         nc.vector.tensor_copy(word_pairs[:], word_pool[:].indirect(offsets[:]))
         k_codes = keep.tile([P, PASSES, SLOTS], U16, name="k_codes", align_bytes=64)
         nc.vector.tensor_copy(k_codes[:], word_pairs[:].bitcast(U16).rearrange("p (i o) -> p o i", o=PASSES))
 
-        grouped = [keep.tile([P, PASSES, QC, PACK], BF16, name=f"grouped{c}", tag=f"grouped{c}", align_bytes=64) for c in range(CHUNKS)]
+        grouped = [
+            keep.tile([P, PASSES, QC, PACK], BF16, name=f"grouped{c}", tag=f"stage{c}", align_bytes=64)[:]
+            for c in range(CHUNKS)
+        ]
         weighted = {}
         summed = keep.tile([P, KB, NQ // HEADS], F32, name="summed")
         scores = {}
@@ -113,7 +122,7 @@ def tile_attend_tok_idxts_topk_kernel(tc, qT, k_words, k_scales, ts, hw, offs, o
             nc.vector.quantize_mx(
                 out=q_codes[:].rearrange("p o q -> p (o q)").bitcast(FP8X4),
                 scales=q_scale[:].rearrange("p o q -> p (o q)"),
-                in_=grouped[c][:].rearrange("p o q t -> p (o q t)"),
+                in_=grouped[c].rearrange("p o q t -> p (o q t)"),
             )
             scores[c] = psum.tile([P, KB, QC], F32, name=f"bank{c}")
             for b in range(KB):
@@ -122,7 +131,7 @@ def tile_attend_tok_idxts_topk_kernel(tc, qT, k_words, k_scales, ts, hw, offs, o
                     nc.tensor.matmul_mx(
                         out=scores[c][:, b, :],
                         lhsT=k_codes[:, o, keys].bitcast(FP4X4),
-                        lhsT_scale=k_scale[:, o, keys],
+                        lhsT_scale=k_scale[o][:, keys],
                         rhs=q_codes[:, o, :].bitcast(FP8X4),
                         rhs_scale=q_scale[:, o, :],
                         start=(o == 0),
@@ -130,7 +139,7 @@ def tile_attend_tok_idxts_topk_kernel(tc, qT, k_words, k_scales, ts, hw, offs, o
                     )
 
         def weigh(c):
-            weighted[c] = keep.tile([P, KB, QC], F32, name="weighted", tag=f"grouped{c + 1}", align_bytes=64)
+            weighted[c] = keep.tile([P, KB, QC], F32, name="weighted", tag=f"stage{c + 1}", align_bytes=64)
             nc.vector.scalar_tensor_tensor(
                 out=weighted[c][:],
                 in0=scores[c][:],
@@ -148,11 +157,10 @@ def tile_attend_tok_idxts_topk_kernel(tc, qT, k_words, k_scales, ts, hw, offs, o
                 op=ALU.add,
             )
 
-        for c in range(CHUNKS):
-            for o in range(PASSES):
-                cast(o, c)
+        for o, c in ((0, 0), (1, 0), (0, 1), (1, 1), (0, 2), (0, 3), (1, 2), (1, 3)):
+            cast(o, c)
         score(0)
-        ts_listed = keep.tile([P, SLOTS], F32, name="ts_listed", tag="grouped0", align_bytes=64)
+        ts_listed = keep.tile([P, SLOTS], F32, name="ts_listed", tag="stage0", align_bytes=64)
         nc.vector.tensor_copy(ts_listed[:], ts_pool[:].indirect(offsets[:]))
         score(1)
         weigh(0)
@@ -171,6 +179,6 @@ def tile_attend_tok_idxts_topk_kernel(tc, qT, k_words, k_scales, ts, hw, offs, o
 
         result = keep.tile([P, KB, NQ // HEADS], F32, name="result")
         nc.vector.tensor_tensor(
-            result[:], summed[:], ts_turned[:, :, 0:1].to_broadcast([P, KB, NQ // HEADS]), ALU.mult
+            result[:], summed[:], ts_turned[:, :, TS_ROW : TS_ROW + 1].to_broadcast([P, KB, NQ // HEADS]), ALU.mult
         )
         nc.sync.dma_start(out[0].rearrange("(b p) j -> p b j", p=P), result[:])

@@ -12,6 +12,7 @@ FP8X4 = mybir.dt.float8_e4m3fn_x4
 FP4X4 = mybir.dt.float4_e2m1fn_x4
 ALU = mybir.AluOpType
 AX = mybir.AxisListType
+COPY = mybir.ActivationFunctionType.Copy
 
 P = 128
 PACK = 4
@@ -43,7 +44,7 @@ def tile_attend_tok_idxts_topk_kernel(tc, qT, k_words, k_scales, ts, hw, offs, o
         raw = {}
 
         def load_q(o, c, n):
-            tile = keep.tile([P, PACK, n * QC], F32, name=f"raw{o}_{c}")
+            tile = keep.tile([P, PACK, n * QC], F32, name=f"raw{o}_{c}", tag=f"raw{o}_{c}")
             rows = qT[0, o * K_PASS : (o + 1) * K_PASS, c * QC : (c + n) * QC]
             nc.sync.dma_start(tile[:], rows.rearrange("(p t) q -> p t q", t=PACK))
             for k in range(n):
@@ -51,7 +52,7 @@ def tile_attend_tok_idxts_topk_kernel(tc, qT, k_words, k_scales, ts, hw, offs, o
 
         word_pool = keep.tile([P, TOKENS], U32, name="word_pool", align_bytes=64)
         words = k_words[0].rearrange("p t b -> p (t b)").bitcast(I32)
-        nc.sync.dma_start(word_pool[:, : TOKENS // 2].bitcast(I32), words[:, : TOKENS // 2])
+        nc.sync.dma_start(word_pool[:, : TOKENS // 4].bitcast(I32), words[:, : TOKENS // 4])
 
         scale_pool = keep.tile([P, TOKENS], U8, name="scale_pool", align_bytes=64)
         nc.vector.memset(scale_pool[:].bitcast(I32), 0)
@@ -61,7 +62,7 @@ def tile_attend_tok_idxts_topk_kernel(tc, qT, k_words, k_scales, ts, hw, offs, o
                 k_scales[:, r:16:4, :].rearrange("o q t -> q o t").bitcast(I32),
             )
 
-        nc.sync.dma_start(word_pool[:, TOKENS // 2 :].bitcast(I32), words[:, TOKENS // 2 :])
+        nc.sync.dma_start(word_pool[:, TOKENS // 4 :].bitcast(I32), words[:, TOKENS // 4 :])
         load_q(0, 0, 1)
         load_q(1, 0, 1)
 
@@ -69,15 +70,15 @@ def tile_attend_tok_idxts_topk_kernel(tc, qT, k_words, k_scales, ts, hw, offs, o
         nc.vector.memset(ts_pool[:].bitcast(I32), 0)
         nc.sync.dma_start(ts_pool[TS_ROW : TS_ROW + 1, :], ts[0:1, :])
 
-        load_q(0, 1, 1)
-        load_q(1, 1, 1)
+        load_q(0, 1, 2)
 
         k_scale = [keep.tile([P, SLOTS], U8, name=f"k_scale{o}", align_bytes=64) for o in range(PASSES)]
         nc.vector.memset(k_scale[1][:].bitcast(I32), 0)
         nc.vector.tensor_copy(k_scale[0][:], scale_pool[:].indirect(offsets[:]))
         nc.sync.dma_start(k_scale[1][0 : P - SHIFT, :].bitcast(I32), k_scale[0][SHIFT:P, :].bitcast(I32))
-        load_q(0, 2, 2)
-        load_q(1, 2, 2)
+        load_q(1, 1, 2)
+        load_q(0, 3, 1)
+        load_q(1, 3, 1)
 
         identity = keep.tile([P, P], F32, name="identity")
         nc.gpsimd.memset(identity[:], 0.0)
@@ -108,6 +109,7 @@ def tile_attend_tok_idxts_topk_kernel(tc, qT, k_words, k_scales, ts, hw, offs, o
         ]
         weighted = {}
         summed = keep.tile([P, KB, NQ // HEADS], F32, name="summed")
+        result = keep.tile([P, KB, NQ // HEADS], F32, name="result")
         scores = {}
 
         def cast(o, c):
@@ -144,25 +146,33 @@ def tile_attend_tok_idxts_topk_kernel(tc, qT, k_words, k_scales, ts, hw, offs, o
                 out=weighted[c][:],
                 in0=scores[c][:],
                 scalar=0.0,
-                in1=hw_all[:, c * QC : (c + 1) * QC].unsqueeze(1).to_broadcast([P, KB, QC]),
+                in1=hw_ts[:] if c == CHUNKS - 1 else hw_all[:, c * QC : (c + 1) * QC].unsqueeze(1).to_broadcast([P, KB, QC]),
                 op0=ALU.max,
                 op1=ALU.mult,
             )
 
         def add_heads(c):
             nc.vector.tensor_reduce(
-                out=summed[:, :, c * RUNS : (c + 1) * RUNS],
+                out=(result if c == CHUNKS - 1 else summed)[:, :, c * RUNS : (c + 1) * RUNS],
                 in_=weighted[c][:].rearrange("p b (j s) -> p b j s", s=HEADS),
                 axis=AX.X,
                 op=ALU.add,
             )
 
-        for o, c in ((0, 0), (1, 0), (0, 1), (1, 1), (0, 2), (0, 3), (1, 2), (1, 3)):
+        for o, c in ((0, 0), (1, 0), (0, 1), (0, 2), (1, 1), (1, 2), (0, 3), (1, 3)):
             cast(o, c)
         score(0)
         ts_listed = keep.tile([P, SLOTS], F32, name="ts_listed", tag="stage0", align_bytes=64)
         nc.vector.tensor_copy(ts_listed[:], ts_pool[:].indirect(offsets[:]))
         score(1)
+        ts_turned = psum.tile([P, KB, P], F32, name="ts_turned")
+        for b in range(KB):
+            nc.tensor.transpose(ts_turned[:, b, :], ts_listed[:, b * P : (b + 1) * P], identity[:])
+        ts_cols = keep.tile([P, KB], F32, name="ts_cols", tag="raw1_3")
+        nc.scalar.copy(ts_cols[:], ts_turned[:, :, TS_ROW])
+        hw_ts = keep.tile([P, KB, QC], F32, name="hw_ts")
+        for b in range(KB):
+            nc.scalar.activation(hw_ts[:, b, :], hw_all[:, NQ - QC :], COPY, scale=ts_cols[:, b : b + 1])
         weigh(0)
         score(2)
         add_heads(0)
@@ -170,15 +180,11 @@ def tile_attend_tok_idxts_topk_kernel(tc, qT, k_words, k_scales, ts, hw, offs, o
         score(3)
         add_heads(1)
         weigh(2)
-        ts_turned = psum.tile([P, KB, P], F32, name="bank2")
-        for b in range(KB):
-            nc.tensor.transpose(ts_turned[:, b, :], ts_listed[:, b * P : (b + 1) * P], identity[:])
         weigh(3)
         add_heads(2)
         add_heads(3)
-
-        result = keep.tile([P, KB, NQ // HEADS], F32, name="result")
-        nc.vector.tensor_tensor(
-            result[:], summed[:], ts_turned[:, :, TS_ROW : TS_ROW + 1].to_broadcast([P, KB, NQ // HEADS]), ALU.mult
+        early = (CHUNKS - 1) * RUNS
+        nc.gpsimd.tensor_tensor(
+            result[:, :, :early], summed[:, :, :early], ts_cols[:].unsqueeze(2).to_broadcast([P, KB, early]), ALU.mult
         )
         nc.sync.dma_start(out[0].rearrange("(b p) j -> p b j", p=P), result[:])

@@ -95,31 +95,52 @@ def tile_attend_tok_idxts_topk_kernel(tc, qT, k_words, k_scales, ts, hw, offs, o
         hw_turned = psum.tile([P, PACK, P], F32, name="hw_turned")
         for c in range(PACK):
             nc.tensor.transpose(hw_turned[:, c, :], hw_rows[:, c : c + 1].to_broadcast([P, P]), identity[:])
-        hw_all = keep.tile([P, NQ], F32, name="hw_all")
-        nc.scalar.copy(hw_all[:].rearrange("m (p c) -> m p c", c=PACK), hw_turned[:].rearrange("m c p -> m p c"))
+        spread = hw_turned[:].rearrange("m c p -> m p c")
+        hw_first = keep.tile([P, QC], F32, name="hw_first", tag="hw_first", align_bytes=64)
+        hw_rest = keep.tile([P, NQ - QC], F32, name="hw_rest")
+        nc.scalar.copy(hw_first[:].rearrange("m (p c) -> m p c", c=PACK), spread[:, : QC // PACK, :])
+        nc.scalar.copy(hw_rest[:].rearrange("m (p c) -> m p c", c=PACK), spread[:, QC // PACK :, :])
+        hw_chunk = [hw_first[:]] + [hw_rest[:, c * QC : (c + 1) * QC] for c in range(CHUNKS - 1)]
 
         word_pairs = keep.tile([P, SLOTS], U32, name="word_pairs", tag="word_pairs", align_bytes=64)
         nc.vector.tensor_copy(word_pairs[:], word_pool[:].indirect(offsets[:]))
         k_codes = keep.tile([P, PASSES, SLOTS], U16, name="k_codes", align_bytes=64)
         nc.vector.tensor_copy(k_codes[:], word_pairs[:].bitcast(U16).rearrange("p (i o) -> p o i", o=PASSES))
 
-        grouped = [
-            keep.tile([P, PASSES, QC, PACK], BF16, name=f"grouped{c}", tag=f"stage{c}", align_bytes=64)[:]
-            for c in range(CHUNKS)
-        ]
+        LAST = CHUNKS - 1
+        grouped = {}
+        for c in range(LAST):
+            both = keep.tile([P, PASSES, QC, PACK], BF16, name=f"grouped{c}", tag=f"stage{c}", align_bytes=64)
+            grouped[c] = both[:]
+            for o in range(PASSES):
+                grouped[o, c] = both[:, o, :, :]
+        for o in range(PASSES):
+            grouped[o, LAST] = keep.tile([P, QC, PACK], BF16, name=f"last{o}", tag=f"last{o}", align_bytes=64)[:]
         weighted = {}
-        summed = keep.tile([P, KB, NQ // HEADS], F32, name="summed")
         result = keep.tile([P, KB, NQ // HEADS], F32, name="result")
         scores = {}
 
         def cast(o, c):
             nc.scalar.copy(
-                grouped[c][:, o, :, :].rearrange("p (g i) t -> p g t i", i=4),
+                grouped[o, c].rearrange("p (g i) t -> p g t i", i=4),
                 raw[o, c].rearrange("p t (g i) -> p g t i", i=4),
             )
 
+        def multiply(bank, b, o, q_codes, q_scale):
+            keys = slice(b * P, (b + 1) * P)
+            nc.tensor.matmul_mx(
+                out=bank,
+                lhsT=k_codes[:, o, keys].bitcast(FP4X4),
+                lhsT_scale=k_scale[o][:, keys],
+                rhs=q_codes.bitcast(FP8X4),
+                rhs_scale=q_scale,
+                start=(o == 0),
+                stop=(o == PASSES - 1),
+            )
+
         def score(c):
-            q_codes = ring.tile([P, PASSES, QC], U32, name="q_codes", align_bytes=64)
+            tag = "hw_first" if c == 1 else f"q_codes{c}"
+            q_codes = keep.tile([P, PASSES, QC], U32, name=f"q_codes{c}", tag=tag, align_bytes=64)
             q_scale = ring.tile([P, PASSES, QC], U8, name="q_scale", align_bytes=64)
             nc.vector.quantize_mx(
                 out=q_codes[:].rearrange("p o q -> p (o q)").bitcast(FP8X4),
@@ -128,42 +149,41 @@ def tile_attend_tok_idxts_topk_kernel(tc, qT, k_words, k_scales, ts, hw, offs, o
             )
             scores[c] = psum.tile([P, KB, QC], F32, name=f"bank{c}")
             for b in range(KB):
-                keys = slice(b * P, (b + 1) * P)
                 for o in range(PASSES):
-                    nc.tensor.matmul_mx(
-                        out=scores[c][:, b, :],
-                        lhsT=k_codes[:, o, keys].bitcast(FP4X4),
-                        lhsT_scale=k_scale[o][:, keys],
-                        rhs=q_codes[:, o, :].bitcast(FP8X4),
-                        rhs_scale=q_scale[:, o, :],
-                        start=(o == 0),
-                        stop=(o == PASSES - 1),
-                    )
+                    multiply(scores[c][:, b, :], b, o, q_codes[:, o, :], q_scale[:, o, :])
+
+        def score_last():
+            codes = []
+            for o in range(PASSES):
+                q_codes = keep.tile([P, QC], U32, name=f"last_codes{o}", align_bytes=64)
+                q_scale = keep.tile([P, QC], U8, name=f"last_scale{o}", align_bytes=64)
+                nc.vector.quantize_mx(
+                    out=q_codes[:].bitcast(FP8X4), scales=q_scale[:], in_=grouped[o, LAST].rearrange("p q t -> p (q t)")
+                )
+                codes.append((q_codes[:], q_scale[:]))
+            banks = [psum.tile([P, 2, QC], F32, name=f"last_bank{h}") for h in range(2)]
+            for b, o in ((0, 0), (2, 0), (0, 1), (1, 0), (1, 1), (2, 1), (3, 0), (3, 1)):
+                multiply(banks[b // 2][:, b % 2, :], b, o, *codes[o])
+            return banks
+
+        def relu_times(target, bank, factors):
+            nc.vector.scalar_tensor_tensor(out=target, in0=bank, scalar=0.0, in1=factors, op0=ALU.max, op1=ALU.mult)
 
         def weigh(c):
-            weighted[c] = keep.tile([P, KB, QC], F32, name="weighted", tag=f"stage{c + 1}", align_bytes=64)
-            nc.vector.scalar_tensor_tensor(
-                out=weighted[c][:],
-                in0=scores[c][:],
-                scalar=0.0,
-                in1=hw_ts[:] if c == CHUNKS - 1 else hw_all[:, c * QC : (c + 1) * QC].unsqueeze(1).to_broadcast([P, KB, QC]),
-                op0=ALU.max,
-                op1=ALU.mult,
-            )
+            tag = ("weighted0", "last0", "last1")[c]
+            weighted[c] = keep.tile([P, KB, QC], F32, name=f"weighted{c}", tag=tag, align_bytes=64)
+            relu_times(weighted[c][:], scores[c][:], hw_chunk[c].unsqueeze(1).to_broadcast([P, KB, QC]))
 
-        def add_heads(c):
-            nc.vector.tensor_reduce(
-                out=(result if c == CHUNKS - 1 else summed)[:, :, c * RUNS : (c + 1) * RUNS],
-                in_=weighted[c][:].rearrange("p b (j s) -> p b j s", s=HEADS),
-                axis=AX.X,
-                op=ALU.add,
-            )
+        def add_heads(c, target):
+            whole = weighted[c][:].rearrange("p b (j s) -> p b j s", s=HEADS)
+            nc.vector.tensor_reduce(out=target[:, :, c * RUNS : (c + 1) * RUNS], in_=whole, axis=AX.X, op=ALU.add)
 
         for o, c in ((0, 0), (1, 0), (0, 1), (0, 2), (1, 1), (1, 2), (0, 3), (1, 3)):
             cast(o, c)
         score(0)
         ts_listed = keep.tile([P, SLOTS], F32, name="ts_listed", tag="stage0", align_bytes=64)
         nc.vector.tensor_copy(ts_listed[:], ts_pool[:].indirect(offsets[:]))
+        weigh(0)
         score(1)
         ts_turned = psum.tile([P, KB, P], F32, name="ts_turned")
         for b in range(KB):
@@ -172,18 +192,20 @@ def tile_attend_tok_idxts_topk_kernel(tc, qT, k_words, k_scales, ts, hw, offs, o
         nc.scalar.copy(ts_cols[:], ts_turned[:, :, TS_ROW])
         hw_ts = keep.tile([P, KB, QC], F32, name="hw_ts")
         for b in range(KB):
-            nc.scalar.activation(hw_ts[:, b, :], hw_all[:, NQ - QC :], COPY, scale=ts_cols[:, b : b + 1])
-        weigh(0)
+            nc.scalar.activation(hw_ts[:, b, :], hw_chunk[LAST], COPY, scale=ts_cols[:, b : b + 1])
         score(2)
-        add_heads(0)
+        summed = keep.tile([P, KB, NQ // HEADS], F32, name="summed", tag="stage2", align_bytes=64)
+        add_heads(0, summed)
+        banks = score_last()
         weigh(1)
-        score(3)
-        add_heads(1)
+        add_heads(1, summed)
         weigh(2)
-        weigh(3)
-        add_heads(2)
-        add_heads(3)
-        early = (CHUNKS - 1) * RUNS
+        weighted[LAST] = keep.tile([P, KB, QC], F32, name="weighted_last")
+        for h in range(2):
+            relu_times(weighted[LAST][:, 2 * h : 2 * h + 2, :], banks[h][:], hw_ts[:, 2 * h : 2 * h + 2, :])
+        add_heads(2, summed)
+        add_heads(LAST, result)
+        early = LAST * RUNS
         nc.gpsimd.tensor_tensor(
             result[:, :, :early], summed[:, :, :early], ts_cols[:].unsqueeze(2).to_broadcast([P, KB, early]), ALU.mult
         )

@@ -172,10 +172,20 @@ def tile_attend_tok_idxts_topk_kernel(tc, qT, k_words, k_scales, ts, hw, offs, o
         def weigh(c):
             tag = ("weighted0", "last0", "last1")[c]
             weighted[c] = keep.tile([P, KB, QC], F32, name=f"weighted{c}", tag=tag, align_bytes=64)
-            relu_times(weighted[c][:], scores[c][:], hw_chunk[c].unsqueeze(1).to_broadcast([P, KB, QC]))
+            factors = hw_ts[c][:] if c == 2 else hw_chunk[c].unsqueeze(1).to_broadcast([P, KB, QC])
+            relu_times(weighted[c][:], scores[c][:], factors)
+
+        pairs = {}
+
+        def pair_heads(c):
+            halves = weighted[c][:].rearrange("p b (j s) -> p (b j) s", s=HEADS)
+            pairs[c] = keep.tile([P, KB * RUNS, HEADS // 2], F32, name=f"pairs{c}")
+            nc.gpsimd.tensor_tensor(pairs[c][:], halves[:, :, : HEADS // 2], halves[:, :, HEADS // 2 :], ALU.add)
 
         def add_heads(c, target):
             whole = weighted[c][:].rearrange("p b (j s) -> p b j s", s=HEADS)
+            if c in pairs:
+                whole = pairs[c][:].rearrange("p (b j) s -> p b j s", b=KB)
             nc.vector.tensor_reduce(out=target[:, :, c * RUNS : (c + 1) * RUNS], in_=whole, axis=AX.X, op=ALU.add)
 
         for o, c in ((0, 0), (1, 0), (0, 1), (0, 2), (1, 1), (1, 2), (0, 3), (1, 3)):
@@ -190,22 +200,26 @@ def tile_attend_tok_idxts_topk_kernel(tc, qT, k_words, k_scales, ts, hw, offs, o
             nc.tensor.transpose(ts_turned[:, b, :], ts_listed[:, b * P : (b + 1) * P], identity[:])
         ts_cols = keep.tile([P, KB], F32, name="ts_cols", tag="raw1_3")
         nc.scalar.copy(ts_cols[:], ts_turned[:, :, TS_ROW])
-        hw_ts = keep.tile([P, KB, QC], F32, name="hw_ts")
-        for b in range(KB):
-            nc.scalar.activation(hw_ts[:, b, :], hw_chunk[LAST], COPY, scale=ts_cols[:, b : b + 1])
+        hw_ts = {}
+        for c in (2, LAST):
+            hw_ts[c] = keep.tile([P, KB, QC], F32, name=f"hw_ts{c}")
+            for b in range(KB):
+                nc.scalar.activation(hw_ts[c][:, b, :], hw_chunk[c], COPY, scale=ts_cols[:, b : b + 1])
         score(2)
         summed = keep.tile([P, KB, NQ // HEADS], F32, name="summed", tag="stage2", align_bytes=64)
         add_heads(0, summed)
         banks = score_last()
         weigh(1)
-        add_heads(1, summed)
+        pair_heads(1)
         weigh(2)
+        pair_heads(2)
         weighted[LAST] = keep.tile([P, KB, QC], F32, name="weighted_last")
         for h in range(2):
-            relu_times(weighted[LAST][:, 2 * h : 2 * h + 2, :], banks[h][:], hw_ts[:, 2 * h : 2 * h + 2, :])
-        add_heads(2, summed)
+            relu_times(weighted[LAST][:, 2 * h : 2 * h + 2, :], banks[h][:], hw_ts[LAST][:, 2 * h : 2 * h + 2, :])
+        add_heads(1, summed)
         add_heads(LAST, result)
-        early = LAST * RUNS
+        add_heads(2, result)
+        early = 2 * RUNS
         nc.gpsimd.tensor_tensor(
             result[:, :, :early], summed[:, :, :early], ts_cols[:].unsqueeze(2).to_broadcast([P, KB, early]), ALU.mult
         )

@@ -21,10 +21,16 @@ K_PASS = P * PACK
 SLOTS, TOKENS, D, NQ, HEADS = 512, 2048, 1024, 512, 16
 QC = 128
 CHUNKS = NQ // QC
+LAST = CHUNKS - 1
 KB = SLOTS // P
 RUNS = QC // HEADS
 SHIFT = 16
 TS_ROW = 8
+QUADRANT = 32
+
+PIECE_BYTES = PACK * QC * 4
+HELD = [(1, 1), (0, 2), (1, 2), (0, 3), (1, 3)]
+SLOT = {piece: n + 1 for n, piece in enumerate(HELD)}
 
 FLOPS = 2 * SLOTS * D * NQ
 
@@ -33,194 +39,183 @@ def tile_attend_tok_idxts_topk_kernel(tc, qT, k_words, k_scales, ts, hw, offs, o
     nc = tc.nc
     with ExitStack() as ctx:
         keep = ctx.enter_context(tc.tile_pool(name="keep", bufs=1))
-        ring = ctx.enter_context(tc.tile_pool(name="ring", bufs=2))
+        shared = ctx.enter_context(tc.tile_pool(name="shared", bufs=1))
         psum = ctx.enter_context(tc.psum_pool(name="psum", bufs=1))
+
+        def sbuf(shape, dtype, name, tag=None):
+            return keep.tile(shape, dtype, name=name, tag=tag or name, align_bytes=64)
+
+        def placed(shape, dtype, name, slot, halves=0):
+            offset = slot * PIECE_BYTES + halves * PIECE_BYTES // 2
+            return shared.tile(shape, dtype, name=name, align_bytes=64, offset=offset)
 
         offsets = keep.tile([P, SLOTS // 16], U16, name="offsets")
         nc.sync.dma_start(offsets[:], offs)
-        hw_rows = keep.tile([P, PACK], F32, name="hw_rows", tag="stage0", align_bytes=64)
+        hw_rows = sbuf([P, PACK], F32, "hw_rows")
         nc.scalar.dma_start(hw_rows[:], hw[0, 0, :].rearrange("(p c) -> p c", c=PACK))
 
         raw = {}
 
-        def load_q(o, c, n):
-            tile = keep.tile([P, PACK, n * QC], F32, name=f"raw{o}_{c}", tag=f"raw{o}_{c}")
-            rows = qT[0, o * K_PASS : (o + 1) * K_PASS, c * QC : (c + n) * QC]
-            nc.sync.dma_start(tile[:], rows.rearrange("(p t) q -> p t q", t=PACK))
-            for k in range(n):
-                raw[o, c + k] = tile[:, :, k * QC : (k + 1) * QC]
+        def load_q(o, c):
+            if (o, c) in SLOT:
+                raw[o, c] = placed([P, PACK, QC], F32, f"raw{o}_{c}", SLOT[o, c])
+            else:
+                raw[o, c] = sbuf([P, PACK, QC], F32, f"raw{o}_{c}")
+            rows = qT[0, o * K_PASS : (o + 1) * K_PASS, c * QC : (c + 1) * QC]
+            nc.sync.dma_start(raw[o, c][:], rows.rearrange("(p t) q -> p t q", t=PACK))
 
-        word_pool = keep.tile([P, TOKENS], U32, name="word_pool", align_bytes=64)
+        word_pool = sbuf([P, TOKENS], U32, "word_pool")
         words = k_words[0].rearrange("p t b -> p (t b)").bitcast(I32)
         nc.sync.dma_start(word_pool[:, : TOKENS // 4].bitcast(I32), words[:, : TOKENS // 4])
 
-        scale_pool = keep.tile([P, TOKENS], U8, name="scale_pool", align_bytes=64)
-        nc.vector.memset(scale_pool[:].bitcast(I32), 0)
+        scale_tile = placed([P, (len(HELD) + 1) * PIECE_BYTES], U8, "scale_tile", 0)
+        scale_pool = scale_tile[:, :TOKENS]
+        nc.vector.memset(scale_pool.bitcast(I32), 0)
         for r in range(4):
             nc.sync.dma_start(
-                scale_pool[r:P:SHIFT, :].bitcast(I32),
+                scale_tile[r:P:SHIFT, :TOKENS].bitcast(I32),
                 k_scales[:, r:16:4, :].rearrange("o q t -> q o t").bitcast(I32),
             )
-
         nc.sync.dma_start(word_pool[:, TOKENS // 4 :].bitcast(I32), words[:, TOKENS // 4 :])
-        load_q(0, 0, 1)
-        load_q(1, 0, 1)
+        load_q(0, 0)
+        load_q(1, 0)
 
-        ts_pool = keep.tile([P, TOKENS], F32, name="ts_pool")
-        nc.vector.memset(ts_pool[:].bitcast(I32), 0)
+        ones = sbuf([P, P], F32, "ones")
+        nc.vector.memset(ones[:], 1.0)
+        column = sbuf([P, P], F32, "column")
+        nc.vector.tensor_tensor_scan(column[:], ones[:], ones[:], 0.0, ALU.mult, ALU.add)
+        turned = sbuf([P, P], F32, "turned")
+        nc.vector.transpose(turned[:], column[:])
+        identity = sbuf([P, P], F32, "identity")
+        for first in range(0, P, QUADRANT):
+            rows = slice(first, first + QUADRANT)
+            nc.vector.tensor_scalar(
+                identity[rows, :], column[rows, :], turned[rows, first : first + 1], None, ALU.is_equal
+            )
+
+        ts_pool = sbuf([P, TOKENS], F32, "ts_pool")
+        for half in range(2):
+            nc.vector.memset(ts_pool[:, half * TOKENS // 2 : (half + 1) * TOKENS // 2].bitcast(I32), 0)
         nc.sync.dma_start(ts_pool[TS_ROW : TS_ROW + 1, :], ts[0:1, :])
-
-        load_q(0, 1, 2)
-
-        k_scale = [keep.tile([P, SLOTS], U8, name=f"k_scale{o}", align_bytes=64) for o in range(PASSES)]
+        load_q(0, 1)
+        k_scale = [sbuf([P, SLOTS], U8, f"k_scale{o}") for o in range(PASSES)]
         nc.vector.memset(k_scale[1][:].bitcast(I32), 0)
-        nc.vector.tensor_copy(k_scale[0][:], scale_pool[:].indirect(offsets[:]))
+        nc.vector.tensor_copy(k_scale[0][:], scale_pool.indirect(offsets[:]))
         nc.sync.dma_start(k_scale[1][0 : P - SHIFT, :].bitcast(I32), k_scale[0][SHIFT:P, :].bitcast(I32))
-        load_q(1, 1, 2)
-        load_q(0, 3, 1)
-        load_q(1, 3, 1)
-
-        identity = keep.tile([P, P], F32, name="identity")
-        nc.gpsimd.memset(identity[:], 0.0)
-        nc.gpsimd.affine_select(
-            out=identity[:],
-            in_=identity[:],
-            compare_op=ALU.not_equal,
-            fill=1.0,
-            base=0,
-            pattern=[[-1, P]],
-            channel_multiplier=1,
-        )
+        load_q(1, 1)
+        for c in range(2, CHUNKS):
+            for o in range(PASSES):
+                load_q(o, c)
 
         hw_turned = psum.tile([P, PACK, P], F32, name="hw_turned")
         for c in range(PACK):
             nc.tensor.transpose(hw_turned[:, c, :], hw_rows[:, c : c + 1].to_broadcast([P, P]), identity[:])
-        spread = hw_turned[:].rearrange("m c p -> m p c")
-        hw_first = keep.tile([P, QC], F32, name="hw_first", tag="hw_first", align_bytes=64)
-        hw_rest = keep.tile([P, NQ - QC], F32, name="hw_rest")
-        nc.scalar.copy(hw_first[:].rearrange("m (p c) -> m p c", c=PACK), spread[:, : QC // PACK, :])
-        nc.scalar.copy(hw_rest[:].rearrange("m (p c) -> m p c", c=PACK), spread[:, QC // PACK :, :])
-        hw_chunk = [hw_first[:]] + [hw_rest[:, c * QC : (c + 1) * QC] for c in range(CHUNKS - 1)]
+        hw_all = sbuf([P, NQ], F32, "hw_all")
+        nc.scalar.copy(hw_all[:].rearrange("m (p c) -> m p c", c=PACK), hw_turned[:].rearrange("m c p -> m p c"))
 
-        word_pairs = keep.tile([P, SLOTS], U32, name="word_pairs", tag="word_pairs", align_bytes=64)
+        word_pairs = sbuf([P, SLOTS], U32, "word_pairs")
         nc.vector.tensor_copy(word_pairs[:], word_pool[:].indirect(offsets[:]))
-        k_codes = keep.tile([P, PASSES, SLOTS], U16, name="k_codes", align_bytes=64)
+        k_codes = sbuf([P, PASSES, SLOTS], U16, "k_codes")
         nc.vector.tensor_copy(k_codes[:], word_pairs[:].bitcast(U16).rearrange("p (i o) -> p o i", o=PASSES))
 
-        LAST = CHUNKS - 1
-        grouped = {}
-        for c in range(LAST):
-            both = keep.tile([P, PASSES, QC, PACK], BF16, name=f"grouped{c}", tag=f"stage{c}", align_bytes=64)
-            grouped[c] = both[:]
-            for o in range(PASSES):
-                grouped[o, c] = both[:, o, :, :]
-        for o in range(PASSES):
-            grouped[o, LAST] = keep.tile([P, QC, PACK], BF16, name=f"last{o}", tag=f"last{o}", align_bytes=64)[:]
-        weighted = {}
-        result = keep.tile([P, KB, NQ // HEADS], F32, name="result")
         scores = {}
+        weighted = {}
+        pairs = {}
 
-        def cast(o, c):
+        def cast(o, c, target):
             nc.scalar.copy(
-                grouped[o, c].rearrange("p (g i) t -> p g t i", i=4),
-                raw[o, c].rearrange("p t (g i) -> p g t i", i=4),
+                target.rearrange("p (g i) t -> p g t i", i=4),
+                raw[o, c][:].rearrange("p t (g i) -> p g t i", i=4),
             )
 
-        def multiply(bank, b, o, q_codes, q_scale):
+        def quantise(source, width, name):
+            q_codes = sbuf([P, width], U32, f"q_codes{name}")
+            q_scale = sbuf([P, width], U8, f"q_scale{name}")
+            nc.vector.quantize_mx(out=q_codes[:].bitcast(FP8X4), scales=q_scale[:], in_=source)
+            return [(q_codes[:, s : s + QC], q_scale[:, s : s + QC]) for s in range(0, width, QC)]
+
+        def multiply(bank, b, o, codes):
             keys = slice(b * P, (b + 1) * P)
             nc.tensor.matmul_mx(
                 out=bank,
                 lhsT=k_codes[:, o, keys].bitcast(FP4X4),
                 lhsT_scale=k_scale[o][:, keys],
-                rhs=q_codes.bitcast(FP8X4),
-                rhs_scale=q_scale,
+                rhs=codes[o][0].bitcast(FP8X4),
+                rhs_scale=codes[o][1],
                 start=(o == 0),
                 stop=(o == PASSES - 1),
             )
 
         def score(c):
-            tag = "hw_first" if c == 1 else f"q_codes{c}"
-            q_codes = keep.tile([P, PASSES, QC], U32, name=f"q_codes{c}", tag=tag, align_bytes=64)
-            q_scale = ring.tile([P, PASSES, QC], U8, name="q_scale", align_bytes=64)
-            nc.vector.quantize_mx(
-                out=q_codes[:].rearrange("p o q -> p (o q)").bitcast(FP8X4),
-                scales=q_scale[:].rearrange("p o q -> p (o q)"),
-                in_=grouped[c].rearrange("p o q t -> p (o q t)"),
-            )
-            scores[c] = psum.tile([P, KB, QC], F32, name=f"bank{c}")
+            grouped = sbuf([P, PASSES, QC, PACK], BF16, f"grouped{c}")
+            for o in range(PASSES):
+                cast(o, c, grouped[:, o, :, :])
+            codes = quantise(grouped[:].rearrange("p o q t -> p (o q t)"), PASSES * QC, c)
+            scores[c] = psum.tile([P, KB, QC], F32, name=f"bank{c}", tag=f"bank{c}")
             for b in range(KB):
                 for o in range(PASSES):
-                    multiply(scores[c][:, b, :], b, o, q_codes[:, o, :], q_scale[:, o, :])
+                    multiply(scores[c][:, b, :], b, o, codes)
 
         def score_last():
             codes = []
             for o in range(PASSES):
-                q_codes = keep.tile([P, QC], U32, name=f"last_codes{o}", align_bytes=64)
-                q_scale = keep.tile([P, QC], U8, name=f"last_scale{o}", align_bytes=64)
-                nc.vector.quantize_mx(
-                    out=q_codes[:].bitcast(FP8X4), scales=q_scale[:], in_=grouped[o, LAST].rearrange("p q t -> p (q t)")
-                )
-                codes.append((q_codes[:], q_scale[:]))
+                grouped = sbuf([P, QC, PACK], BF16, f"last{o}")
+                cast(o, LAST, grouped[:])
+                codes.extend(quantise(grouped[:].rearrange("p q t -> p (q t)"), QC, f"last{o}"))
             banks = [psum.tile([P, 2, QC], F32, name=f"last_bank{h}") for h in range(2)]
             for b, o in ((0, 0), (2, 0), (0, 1), (1, 0), (1, 1), (2, 1), (3, 0), (3, 1)):
-                multiply(banks[b // 2][:, b % 2, :], b, o, *codes[o])
+                multiply(banks[b // 2][:, b % 2, :], b, o, codes)
             return banks
 
         def relu_times(target, bank, factors):
             nc.vector.scalar_tensor_tensor(out=target, in0=bank, scalar=0.0, in1=factors, op0=ALU.max, op1=ALU.mult)
 
-        def weigh(c):
-            tag = ("weighted0", "last0", "last1")[c]
-            weighted[c] = keep.tile([P, KB, QC], F32, name=f"weighted{c}", tag=tag, align_bytes=64)
-            factors = hw_ts[c][:] if c == 2 else hw_chunk[c].unsqueeze(1).to_broadcast([P, KB, QC])
-            relu_times(weighted[c][:], scores[c][:], factors)
+        def weigh(c, target):
+            weighted[c] = target
+            factors = hw_all[:, c * QC : (c + 1) * QC].unsqueeze(1).to_broadcast([P, KB, QC])
+            relu_times(target, scores[c][:], factors)
 
-        pairs = {}
-
-        def pair_heads(c):
-            halves = weighted[c][:].rearrange("p b (j s) -> p (b j) s", s=HEADS)
-            pairs[c] = keep.tile([P, KB * RUNS, HEADS // 2], F32, name=f"pairs{c}")
+        def pair_heads(c, tag=None):
+            halves = weighted[c].rearrange("p b (j s) -> p (b j) s", s=HEADS)
+            pairs[c] = sbuf([P, KB * RUNS, HEADS // 2], F32, f"pairs{c}", tag)
             nc.gpsimd.tensor_tensor(pairs[c][:], halves[:, :, : HEADS // 2], halves[:, :, HEADS // 2 :], ALU.add)
 
         def add_heads(c, target):
-            whole = weighted[c][:].rearrange("p b (j s) -> p b j s", s=HEADS)
+            whole = weighted[c].rearrange("p b (j s) -> p b j s", s=HEADS)
             if c in pairs:
                 whole = pairs[c][:].rearrange("p (b j) s -> p b j s", b=KB)
             nc.vector.tensor_reduce(out=target[:, :, c * RUNS : (c + 1) * RUNS], in_=whole, axis=AX.X, op=ALU.add)
 
-        for o, c in ((0, 0), (1, 0), (0, 1), (0, 2), (1, 1), (1, 2), (0, 3), (1, 3)):
-            cast(o, c)
         score(0)
-        ts_listed = keep.tile([P, SLOTS], F32, name="ts_listed", tag="stage0", align_bytes=64)
+        ts_listed = sbuf([P, SLOTS], F32, "ts_listed", "raw1_0")
         nc.vector.tensor_copy(ts_listed[:], ts_pool[:].indirect(offsets[:]))
-        weigh(0)
         score(1)
-        ts_turned = psum.tile([P, KB, P], F32, name="ts_turned")
+        weigh(0, placed([P, KB, QC], F32, "weighted0", SLOT[1, 1])[:])
+        ts_turned = psum.tile([P, KB, P], F32, name="ts_turned", tag="bank0")
         for b in range(KB):
             nc.tensor.transpose(ts_turned[:, b, :], ts_listed[:, b * P : (b + 1) * P], identity[:])
-        ts_cols = keep.tile([P, KB], F32, name="ts_cols", tag="raw1_3")
-        nc.scalar.copy(ts_cols[:], ts_turned[:, :, TS_ROW])
-        hw_ts = {}
-        for c in (2, LAST):
-            hw_ts[c] = keep.tile([P, KB, QC], F32, name=f"hw_ts{c}")
-            for b in range(KB):
-                nc.scalar.activation(hw_ts[c][:, b, :], hw_chunk[c], COPY, scale=ts_cols[:, b : b + 1])
         score(2)
-        summed = keep.tile([P, KB, NQ // HEADS], F32, name="summed", tag="stage2", align_bytes=64)
+        summed = placed([P, KB, LAST * RUNS], F32, "summed", SLOT[1, 2], 1)
         add_heads(0, summed)
+        weigh(1, placed([P, KB, QC], F32, "weighted1", SLOT[0, 2], 1)[:])
         banks = score_last()
-        weigh(1)
-        pair_heads(1)
-        weigh(2)
+        ts_cols = placed([P, KB], F32, "ts_cols", SLOT[0, 3])[:]
+        nc.scalar.copy(ts_cols, ts_turned[:, :, TS_ROW])
+        hw_ts = placed([P, KB, QC], F32, "hw_ts", SLOT[1, 3], 1)
+        for b in range(KB):
+            nc.scalar.activation(hw_ts[:, b, :], hw_all[:, LAST * QC :], COPY, scale=ts_cols[:, b : b + 1])
+        pair_heads(1, "last1")
+        weigh(2, placed([P, KB, QC], F32, "weighted2", SLOT[0, 3], 1)[:])
         pair_heads(2)
-        weighted[LAST] = keep.tile([P, KB, QC], F32, name="weighted_last")
-        for h in range(2):
-            relu_times(weighted[LAST][:, 2 * h : 2 * h + 2, :], banks[h][:], hw_ts[LAST][:, 2 * h : 2 * h + 2, :])
+        weighted[LAST] = sbuf([P, KB, QC], F32, "weighted_last")[:]
+        relu_times(weighted[LAST][:, :2, :], banks[0][:], hw_ts[:, :2, :])
         add_heads(1, summed)
+        relu_times(weighted[LAST][:, 2:, :], banks[1][:], hw_ts[:, 2:, :])
+        add_heads(2, summed)
+        result = placed([P, KB, NQ // HEADS], F32, "result", SLOT[0, 3], 1)
         add_heads(LAST, result)
-        add_heads(2, result)
-        early = 2 * RUNS
+        early = LAST * RUNS
         nc.gpsimd.tensor_tensor(
-            result[:, :, :early], summed[:, :, :early], ts_cols[:].unsqueeze(2).to_broadcast([P, KB, early]), ALU.mult
+            result[:, :, :early], summed[:], ts_cols.unsqueeze(2).to_broadcast([P, KB, early]), ALU.mult
         )
         nc.sync.dma_start(out[0].rearrange("(b p) j -> p b j", p=P), result[:])

@@ -176,14 +176,14 @@ def tile_attend_tok_idxts_topk_kernel(tc, qT, k_words, k_scales, ts, hw, offs, o
             relu_times(target, scores[c][:], factors)
 
         def pair_heads(c, tag=None):
-            halves = weighted[c].rearrange("p b (j s) -> p (b j) s", s=HEADS)
-            pairs[c] = sbuf([P, KB * RUNS, HEADS // 2], F32, f"pairs{c}", tag)
-            nc.gpsimd.tensor_tensor(pairs[c][:], halves[:, :, : HEADS // 2], halves[:, :, HEADS // 2 :], ALU.add)
+            neighbours = weighted[c].rearrange("p b (m e) -> p (b m) e", e=2)
+            pairs[c] = sbuf([P, KB * QC // 2], F32, f"pairs{c}", tag)
+            nc.gpsimd.tensor_tensor(pairs[c][:], neighbours[:, :, 0], neighbours[:, :, 1], ALU.add)
 
         def add_heads(c, target):
             whole = weighted[c].rearrange("p b (j s) -> p b j s", s=HEADS)
             if c in pairs:
-                whole = pairs[c][:].rearrange("p (b j) s -> p b j s", b=KB)
+                whole = pairs[c][:].rearrange("p (b j s) -> p b j s", b=KB, j=RUNS)
             nc.vector.tensor_reduce(out=target[:, :, c * RUNS : (c + 1) * RUNS], in_=whole, axis=AX.X, op=ALU.add)
 
         score(0)

@@ -101,7 +101,11 @@ def tile_attend_tok_idxts_topk_kernel(tc, qT, k_words, k_scales, ts, hw, offs, o
         k_scale = [sbuf([P, SLOTS], U8, f"k_scale{o}") for o in range(PASSES)]
         nc.vector.memset(k_scale[1][:].bitcast(I32), 0)
         nc.vector.tensor_copy(k_scale[0][:], scale_pool.indirect(offsets[:]))
-        nc.sync.dma_start(k_scale[1][0 : P - SHIFT, :].bitcast(I32), k_scale[0][SHIFT:P, :].bitcast(I32))
+        for first, rows in ((0, 64), (64, 4), (96, 4)):
+            nc.sync.dma_start(
+                k_scale[1][first : first + rows, :].bitcast(I32),
+                k_scale[0][first + SHIFT : first + SHIFT + rows, :].bitcast(I32),
+            )
         load_q(1, 1)
         for c in range(2, CHUNKS):
             for o in range(PASSES):

@@ -25,12 +25,11 @@ LAST = CHUNKS - 1
 KB = SLOTS // P
 RUNS = QC // HEADS
 SHIFT = 16
-TS_ROW = 8
+TS_ROW = P - 1
 QUADRANT = 32
-
+HALF = SLOTS // 2
+ALIGN = 256
 PIECE_BYTES = PACK * QC * 4
-HELD = [(1, 1), (0, 2), (1, 2), (0, 3), (1, 3)]
-SLOT = {piece: n + 1 for n, piece in enumerate(HELD)}
 
 FLOPS = 2 * SLOTS * D * NQ
 
@@ -39,36 +38,37 @@ def tile_attend_tok_idxts_topk_kernel(tc, qT, k_words, k_scales, ts, hw, offs, o
     nc = tc.nc
     with ExitStack() as ctx:
         keep = ctx.enter_context(tc.tile_pool(name="keep", bufs=1))
-        shared = ctx.enter_context(tc.tile_pool(name="shared", bufs=1))
+        main = ctx.enter_context(tc.tile_pool(name="main", bufs=1))
         psum = ctx.enter_context(tc.psum_pool(name="psum", bufs=1))
+        place = {"free": 0}
 
-        def sbuf(shape, dtype, name, tag=None):
-            return keep.tile(shape, dtype, name=name, tag=tag or name, align_bytes=64)
-
-        def placed(shape, dtype, name, slot, halves=0):
-            offset = slot * PIECE_BYTES + halves * PIECE_BYTES // 2
-            return shared.tile(shape, dtype, name=name, align_bytes=64, offset=offset)
+        def sbuf(shape, dtype, size, name, at=None):
+            if at is None:
+                at = place["free"]
+                place["free"] = at + (size + ALIGN - 1) // ALIGN * ALIGN
+            place[name] = at
+            return main.tile(shape, dtype, name=name, align_bytes=ALIGN, offset=at)
 
         offsets = keep.tile([P, SLOTS // 16], U16, name="offsets")
         nc.sync.dma_start(offsets[:], offs)
-        hw_rows = sbuf([P, PACK], F32, "hw_rows")
-        nc.scalar.dma_start(hw_rows[:], hw[0, 0, :].rearrange("(p c) -> p c", c=PACK))
 
         raw = {}
 
-        def load_q(o, c):
-            if (o, c) in SLOT:
-                raw[o, c] = placed([P, PACK, QC], F32, f"raw{o}_{c}", SLOT[o, c])
-            else:
-                raw[o, c] = sbuf([P, PACK, QC], F32, f"raw{o}_{c}")
-            rows = qT[0, o * K_PASS : (o + 1) * K_PASS, c * QC : (c + 1) * QC]
-            nc.sync.dma_start(raw[o, c][:], rows.rearrange("(p t) q -> p t q", t=PACK))
+        def load_q(o, c, chunks=1, at=None):
+            piece = sbuf([P, PACK, chunks * QC], F32, chunks * PIECE_BYTES, f"raw{o}_{c}", at)
+            rows = qT[0, o * K_PASS : (o + 1) * K_PASS, c * QC : (c + chunks) * QC]
+            nc.sync.dma_start(piece[:], rows.rearrange("(p t) q -> p t q", t=PACK))
+            for n in range(chunks):
+                raw[o, c + n] = piece[:, :, n * QC : (n + 1) * QC]
 
-        word_pool = sbuf([P, TOKENS], U32, "word_pool")
-        words = k_words[0].rearrange("p t b -> p (t b)").bitcast(I32)
-        nc.sync.dma_start(word_pool[:, : TOKENS // 4].bitcast(I32), words[:, : TOKENS // 4])
+        ts_pool = sbuf([P, TOKENS], F32, TOKENS * 4, "ts_pool")
+        nc.sync.dma_start(ts_pool[TS_ROW:, :], ts[0:1, :])
+        load_q(0, 0, 2)
+        hw_rows = sbuf([P, PACK], F32, PACK * 4, "hw_rows")
+        nc.scalar.dma_start(hw_rows[:], hw[0, 0, :].rearrange("(p c) -> p c", c=PACK))
 
-        scale_tile = placed([P, (len(HELD) + 1) * PIECE_BYTES], U8, "scale_tile", 0)
+        late = [(0, 2), (1, 2), (0, 3), (1, 3)]
+        scale_tile = sbuf([P, (len(late) + 1) * PIECE_BYTES], U8, (len(late) + 1) * PIECE_BYTES, "scale_tile")
         scale_pool = scale_tile[:, :TOKENS]
         nc.vector.memset(scale_pool.bitcast(I32), 0)
         for r in range(4):
@@ -76,29 +76,26 @@ def tile_attend_tok_idxts_topk_kernel(tc, qT, k_words, k_scales, ts, hw, offs, o
                 scale_tile[r:P:SHIFT, :TOKENS].bitcast(I32),
                 k_scales[:, r:16:4, :].rearrange("o q t -> q o t").bitcast(I32),
             )
-        nc.sync.dma_start(word_pool[:, TOKENS // 4 :].bitcast(I32), words[:, TOKENS // 4 :])
-        load_q(0, 0)
+        word_pool = sbuf([P, TOKENS], U32, TOKENS * 4, "word_pool")
+        nc.sync.dma_start(word_pool[:].bitcast(I32), k_words[0].rearrange("p t b -> p (t b)").bitcast(I32))
         load_q(1, 0)
+        load_q(1, 1)
 
-        ones = sbuf([P, P], F32, "ones")
+        nc.vector.memset(ts_pool[:TS_ROW, :].bitcast(I32), 0)
+        ones = sbuf([P, P], F32, P * 4, "ones")
         nc.vector.memset(ones[:], 1.0)
-        column = sbuf([P, P], F32, "column")
+        column = sbuf([P, P], F32, P * 4, "column")
         nc.vector.tensor_tensor_scan(column[:], ones[:], ones[:], 0.0, ALU.mult, ALU.add)
-        turned = sbuf([P, P], F32, "turned")
+        turned = sbuf([P, P], F32, P * 4, "turned")
         nc.vector.transpose(turned[:], column[:])
-        identity = sbuf([P, P], F32, "identity")
+        identity = sbuf([P, P], F32, P * 4, "identity")
         for first in range(0, P, QUADRANT):
             rows = slice(first, first + QUADRANT)
             nc.vector.tensor_scalar(
                 identity[rows, :], column[rows, :], turned[rows, first : first + 1], None, ALU.is_equal
             )
 
-        ts_pool = sbuf([P, TOKENS], F32, "ts_pool")
-        for half in range(2):
-            nc.vector.memset(ts_pool[:, half * TOKENS // 2 : (half + 1) * TOKENS // 2].bitcast(I32), 0)
-        nc.sync.dma_start(ts_pool[TS_ROW : TS_ROW + 1, :], ts[0:1, :])
-        load_q(0, 1)
-        k_scale = [sbuf([P, SLOTS], U8, f"k_scale{o}") for o in range(PASSES)]
+        k_scale = [sbuf([P, SLOTS], U8, SLOTS, f"k_scale{o}") for o in range(PASSES)]
         nc.vector.memset(k_scale[1][:].bitcast(I32), 0)
         nc.vector.tensor_copy(k_scale[0][:], scale_pool.indirect(offsets[:]))
         for first, rows in ((0, 64), (64, 4), (96, 4)):
@@ -106,120 +103,166 @@ def tile_attend_tok_idxts_topk_kernel(tc, qT, k_words, k_scales, ts, hw, offs, o
                 k_scale[1][first : first + rows, :].bitcast(I32),
                 k_scale[0][first + SHIFT : first + SHIFT + rows, :].bitcast(I32),
             )
-        load_q(1, 1)
-        for c in range(2, CHUNKS):
-            for o in range(PASSES):
-                load_q(o, c)
+        for n, (o, c) in enumerate(late):
+            load_q(o, c, 1, place["scale_tile"] + (n + 1) * PIECE_BYTES)
 
+        codes = {}
+
+        def cast(o, c, target, copy=nc.scalar.copy):
+            copy(target.rearrange("p (g i) t -> p g t i", i=4), raw[o, c].rearrange("p t (g i) -> p g t i", i=4))
+
+        def cast_pass(o, c, copy=nc.scalar.copy):
+            grouped = sbuf([P, QC, PACK], BF16, QC * PACK * 2, f"grouped{o}_{c}")
+            cast(o, c, grouped[:], copy)
+            return grouped[:].rearrange("p q t -> p (q t)")
+
+        def quantise(source, passes, at=None):
+            width = len(passes) * QC
+            name = f"{passes[0][0]}_{passes[0][1]}"
+            q_codes = sbuf([P, width], U32, width * 4, f"q_codes{name}", at)
+            q_scale = sbuf([P, width], U8, width, f"q_scale{name}")
+            nc.vector.quantize_mx(out=q_codes[:].bitcast(FP8X4), scales=q_scale[:], in_=source)
+            for n, piece in enumerate(passes):
+                codes[piece] = (q_codes[:, n * QC : (n + 1) * QC], q_scale[:, n * QC : (n + 1) * QC])
+
+        hw_wide = sbuf([P, PACK, P], F32, PACK * P * 4, "hw_wide")
+        nc.scalar.copy(hw_wide[:], hw_rows[:].unsqueeze(2).to_broadcast([P, PACK, P]))
         hw_turned = psum.tile([P, PACK, P], F32, name="hw_turned")
         for c in range(PACK):
-            nc.tensor.transpose(hw_turned[:, c, :], hw_rows[:, c : c + 1].to_broadcast([P, P]), identity[:])
-        hw_all = sbuf([P, NQ], F32, "hw_all")
-        nc.scalar.copy(hw_all[:].rearrange("m (p c) -> m p c", c=PACK), hw_turned[:].rearrange("m c p -> m p c"))
+            nc.tensor.transpose(hw_turned[:, c, :], hw_wide[:, c, :], identity[:])
+        hw_spread = hw_turned[:].rearrange("m c p -> m p c")
 
-        word_pairs = sbuf([P, SLOTS], U32, "word_pairs")
-        nc.vector.tensor_copy(word_pairs[:], word_pool[:].indirect(offsets[:]))
-        k_codes = sbuf([P, PASSES, SLOTS], U16, "k_codes")
-        nc.vector.tensor_copy(k_codes[:], word_pairs[:].bitcast(U16).rearrange("p (i o) -> p o i", o=PASSES))
+        ts_listed = sbuf([P, SLOTS], F32, SLOTS * 4, "ts_listed")
+        nc.scalar.activation(ts_listed[:], ts_pool[:].indirect(offsets[:]), COPY)
+        quantise(cast_pass(0, 0, nc.vector.tensor_copy), [(0, 0)], place["scale_tile"])
+        ahead = cast_pass(0, 1, nc.vector.tensor_copy)
+        early = LAST * QC
+        hw_early = sbuf([P, early], F32, early * 4, "hw_early", place["ts_pool"])
+        nc.scalar.copy(hw_early[:].rearrange("m (p c) -> m p c", c=PACK), hw_spread[:, : early // PACK, :])
 
-        scores = {}
-        weighted = {}
-        pairs = {}
-
-        def cast(o, c, target):
-            nc.scalar.copy(
-                target.rearrange("p (g i) t -> p g t i", i=4),
-                raw[o, c][:].rearrange("p t (g i) -> p g t i", i=4),
-            )
-
-        def quantise(source, width, name):
-            q_codes = sbuf([P, width], U32, f"q_codes{name}")
-            q_scale = sbuf([P, width], U8, f"q_scale{name}")
-            nc.vector.quantize_mx(out=q_codes[:].bitcast(FP8X4), scales=q_scale[:], in_=source)
-            return [(q_codes[:, s : s + QC], q_scale[:, s : s + QC]) for s in range(0, width, QC)]
-
-        def multiply(bank, b, o, codes):
-            keys = slice(b * P, (b + 1) * P)
-            nc.tensor.matmul_mx(
-                out=bank,
-                lhsT=k_codes[:, o, keys].bitcast(FP4X4),
-                lhsT_scale=k_scale[o][:, keys],
-                rhs=codes[o][0].bitcast(FP8X4),
-                rhs_scale=codes[o][1],
-                start=(o == 0),
-                stop=(o == PASSES - 1),
-            )
-
-        def score(c):
-            grouped = sbuf([P, PASSES, QC, PACK], BF16, f"grouped{c}")
-            for o in range(PASSES):
-                cast(o, c, grouped[:, o, :, :])
-            codes = quantise(grouped[:].rearrange("p o q t -> p (o q t)"), PASSES * QC, c)
-            scores[c] = psum.tile([P, KB, QC], F32, name=f"bank{c}", tag=f"bank{c}")
-            for b in range(KB):
-                for o in range(PASSES):
-                    multiply(scores[c][:, b, :], b, o, codes)
-
-        def score_last():
-            codes = []
-            for o in range(PASSES):
-                grouped = sbuf([P, QC, PACK], BF16, f"last{o}")
-                cast(o, LAST, grouped[:])
-                codes.extend(quantise(grouped[:].rearrange("p q t -> p (q t)"), QC, f"last{o}"))
-            banks = [psum.tile([P, 2, QC], F32, name=f"last_bank{h}") for h in range(2)]
-            for b, o in ((0, 0), (2, 0), (0, 1), (1, 0), (1, 1), (2, 1), (3, 0), (3, 1)):
-                multiply(banks[b // 2][:, b % 2, :], b, o, codes)
-            return banks
-
-        def relu_times(target, bank, factors):
-            nc.vector.scalar_tensor_tensor(out=target, in0=bank, scalar=0.0, in1=factors, op0=ALU.max, op1=ALU.mult)
-
-        def weigh(c, target):
-            weighted[c] = target
-            factors = hw_all[:, c * QC : (c + 1) * QC].unsqueeze(1).to_broadcast([P, KB, QC])
-            relu_times(target, scores[c][:], factors)
-
-        def pair_heads(c, tag=None):
-            neighbours = weighted[c].rearrange("p b (m e) -> p (b m) e", e=2)
-            pairs[c] = sbuf([P, KB * QC // 2], F32, f"pairs{c}", tag)
-            nc.gpsimd.tensor_tensor(pairs[c][:], neighbours[:, :, 0], neighbours[:, :, 1], ALU.add)
-
-        def add_heads(c, target):
-            whole = weighted[c].rearrange("p b (j s) -> p b j s", s=HEADS)
-            if c in pairs:
-                whole = pairs[c][:].rearrange("p (b j s) -> p b j s", b=KB, j=RUNS)
-            nc.vector.tensor_reduce(out=target[:, :, c * RUNS : (c + 1) * RUNS], in_=whole, axis=AX.X, op=ALU.add)
-
-        score(0)
-        ts_listed = sbuf([P, SLOTS], F32, "ts_listed", "raw1_0")
-        nc.vector.tensor_copy(ts_listed[:], ts_pool[:].indirect(offsets[:]))
-        score(1)
-        weigh(0, placed([P, KB, QC], F32, "weighted0", SLOT[1, 1])[:])
-        ts_turned = psum.tile([P, KB, P], F32, name="ts_turned", tag="bank0")
+        ts_turned = psum.tile([P, KB, P], F32, name="ts_turned")
         for b in range(KB):
             nc.tensor.transpose(ts_turned[:, b, :], ts_listed[:, b * P : (b + 1) * P], identity[:])
-        score(2)
-        summed = placed([P, KB, LAST * RUNS], F32, "summed", SLOT[1, 2], 1)
-        add_heads(0, summed)
-        weigh(1, placed([P, KB, QC], F32, "weighted1", SLOT[0, 2], 1)[:])
-        banks = score_last()
-        ts_cols = placed([P, KB], F32, "ts_cols", SLOT[0, 3])[:]
-        nc.scalar.copy(ts_cols, ts_turned[:, :, TS_ROW])
-        hw_ts = placed([P, KB, QC], F32, "hw_ts", SLOT[1, 3], 1)
+        ts_cols = sbuf([P, KB], F32, KB * 4, "ts_cols")
+        nc.scalar.copy(ts_cols[:], ts_turned[:, :, TS_ROW])
+        hw_ts = sbuf([P, KB, QC], F32, KB * QC * 4, "hw_ts")
         for b in range(KB):
-            nc.scalar.activation(hw_ts[:, b, :], hw_all[:, LAST * QC :], COPY, scale=ts_cols[:, b : b + 1])
-        pair_heads(1, "last1")
-        weigh(2, placed([P, KB, QC], F32, "weighted2", SLOT[0, 3], 1)[:])
-        pair_heads(2)
-        weighted[LAST] = sbuf([P, KB, QC], F32, "weighted_last")[:]
-        relu_times(weighted[LAST][:, :2, :], banks[0][:], hw_ts[:, :2, :])
-        add_heads(1, summed)
-        relu_times(weighted[LAST][:, 2:, :], banks[1][:], hw_ts[:, 2:, :])
-        add_heads(2, summed)
-        result = placed([P, KB, NQ // HEADS], F32, "result", SLOT[0, 3], 1)
-        add_heads(LAST, result)
-        early = LAST * RUNS
+            nc.scalar.activation(
+                hw_ts[:, b, :].rearrange("m (p c) -> m p c", c=PACK),
+                hw_spread[:, early // PACK :, :],
+                COPY,
+                scale=ts_cols[:, b : b + 1],
+            )
+
+        def factors(blocks, c):
+            if c == LAST:
+                return hw_ts[:, blocks.start : blocks.stop, :]
+            return hw_early[:, c * QC : (c + 1) * QC].unsqueeze(1).to_broadcast([P, len(blocks), QC])
+
+        word_pairs = []
+        for h in range(2):
+            word_pairs.append(sbuf([P, HALF], U32, HALF * 4, f"word_pairs{h}"))
+            listed = offsets[:, h * HALF // 16 : (h + 1) * HALF // 16]
+            nc.vector.tensor_copy(word_pairs[h][:], word_pool[:].indirect(listed))
+        k_codes = []
+
+        def split(h):
+            k_codes.append(sbuf([P, PASSES, HALF], U16, PASSES * HALF * 2, f"k_codes{h}"))
+            nc.vector.tensor_copy(
+                k_codes[h][:], word_pairs[h][:].bitcast(U16).rearrange("p (i o) -> p o i", o=PASSES)
+            )
+
+        def multiply(bank, b, o, c, start, stop):
+            nc.tensor.matmul_mx(
+                out=bank,
+                lhsT=k_codes[b // 2][:, o, (b % 2) * P : (b % 2 + 1) * P].bitcast(FP4X4),
+                lhsT_scale=k_scale[o][:, b * P : (b + 1) * P],
+                rhs=codes[o, c][0].bitcast(FP8X4),
+                rhs_scale=codes[o, c][1],
+                start=start,
+                stop=stop,
+            )
+
+        def one_pass(bank, blocks, o, c):
+            for n, b in enumerate(blocks):
+                multiply(bank[:, n, :], b, o, c, o == 0 and n == 0, o == PASSES - 1 and n == len(blocks) - 1)
+
+        def weigh(target, bank, blocks, c):
+            nc.vector.scalar_tensor_tensor(
+                out=target[:, blocks.start : blocks.stop, :],
+                in0=bank[:],
+                scalar=0.0,
+                in1=factors(blocks, c),
+                op0=ALU.max,
+                op1=ALU.mult,
+            )
+
+        def pair_heads(c, source, at):
+            neighbours = source.rearrange("p b (m e) -> p (b m) e", e=2)
+            pairs = sbuf([P, KB, QC // 2], F32, KB * QC * 2, f"pairs{c}", at)
+            flat = pairs[:].rearrange("p b m -> p (b m)")
+            nc.gpsimd.tensor_tensor(flat, neighbours[:, :, 0], neighbours[:, :, 1], ALU.add)
+            return pairs
+
+        def add_heads(target, source, blocks, c):
+            nc.vector.tensor_reduce(
+                out=target[:, blocks.start : blocks.stop, c * RUNS : (c + 1) * RUNS],
+                in_=source[:, blocks.start : blocks.stop, :].rearrange("p b (j s) -> p b j s", j=RUNS),
+                axis=AX.X,
+                op=ALU.add,
+            )
+
+        def weigh_into(c, at):
+            return sbuf([P, KB, QC], F32, KB * QC * 4, f"weighted{c}", at)
+
+        halves = [range(0, KB // 2), range(KB // 2, KB)]
+        whole = range(KB)
+        first_banks = [psum.tile([P, 2, QC], F32, name=f"first_bank{h}") for h in range(2)]
+        banks = {c: psum.tile([P, KB, QC], F32, name=f"bank{c}") for c in (1, 2)}
+        last_banks = [psum.tile([P, 2, QC], F32, name=f"last_bank{h}") for h in range(2)]
+        for h in range(2):
+            split(h)
+            one_pass(first_banks[h], halves[h], 0, 0)
+        quantise(cast_pass(1, 0), [(1, 0)], place["word_pool"])
+        for h in range(2):
+            one_pass(first_banks[h], halves[h], 1, 0)
+        quantise(ahead, [(0, 1)], place["raw1_0"])
+        one_pass(banks[1], whole, 0, 1)
+        quantise(cast_pass(1, 1), [(1, 1)], place["word_pool"] + PIECE_BYTES)
+        one_pass(banks[1], whole, 1, 1)
+        weighted0 = weigh_into(0, None)
+        for h in range(2):
+            weigh(weighted0, first_banks[h], halves[h], 0)
+        quantise(cast_pass(0, 2), [(0, 2)], place["q_codes1_0"])
+        one_pass(banks[2], whole, 0, 2)
+        pairs0 = pair_heads(0, weighted0[:], place["grouped0_2"])
+        weighted1 = weigh_into(1, place["raw0_2"])
+        weigh(weighted1, banks[1], whole, 1)
+        quantise(cast_pass(1, 2), [(1, 2)], place["q_codes1_1"])
+        one_pass(banks[2], whole, 1, 2)
+        summed = sbuf([P, KB, LAST * RUNS], F32, KB * LAST * RUNS * 4, "summed", place["raw1_2"])
+        add_heads(summed, pairs0, whole, 0)
+        add_heads(summed, weighted1, whole, 1)
+        quantise(cast_pass(0, LAST), [(0, LAST)], place["pairs0"])
+        for h in range(2):
+            one_pass(last_banks[h], halves[h], 0, LAST)
+        weighted2 = weigh_into(2, place["raw0_3"])
+        weigh(weighted2, banks[2], whole, 2)
+        quantise(cast_pass(1, LAST), [(1, LAST)], place["q_codes1_2"])
+        for h in range(2):
+            one_pass(last_banks[h], halves[h], 1, LAST)
+        add_heads(summed, weighted2, whole, 2)
+        result = sbuf([P, KB, NQ // HEADS], F32, KB * NQ // HEADS * 4, "result")
         nc.gpsimd.tensor_tensor(
-            result[:, :, :early], summed[:], ts_cols.unsqueeze(2).to_broadcast([P, KB, early]), ALU.mult
+            result[:, :, : LAST * RUNS],
+            summed[:],
+            ts_cols[:].unsqueeze(2).to_broadcast([P, KB, LAST * RUNS]),
+            ALU.mult,
         )
-        nc.sync.dma_start(out[0].rearrange("(b p) j -> p b j", p=P), result[:])
+        weighted3 = weigh_into(LAST, None)
+        for h in range(2):
+            weigh(weighted3, last_banks[h], halves[h], LAST)
+        rows = out[0].rearrange("(b p) j -> p b j", p=P)
+        for blocks in halves:
+            add_heads(result, weighted3, blocks, LAST)
+            nc.sync.dma_start(rows[:, blocks.start : blocks.stop, :], result[:, blocks.start : blocks.stop, :])

@@ -28,6 +28,7 @@ SHIFT = 16
 TS_ROW = P - 1
 QUADRANT = 32
 HALF = SLOTS // 2
+AHEAD = TOKENS // 4
 ALIGN = 256
 PIECE_BYTES = PACK * QC * 4
 
@@ -61,27 +62,30 @@ def tile_attend_tok_idxts_topk_kernel(tc, qT, k_words, k_scales, ts, hw, offs, o
             for n in range(chunks):
                 raw[o, c + n] = piece[:, :, n * QC : (n + 1) * QC]
 
+        word_pool = sbuf([P, TOKENS], U32, TOKENS * 4, "word_pool")
+        words = k_words[0].rearrange("p t b -> p (t b)").bitcast(I32)
+        nc.sync.dma_start(word_pool[:, :AHEAD].bitcast(I32), words[:, :AHEAD])
         ts_pool = sbuf([P, TOKENS], F32, TOKENS * 4, "ts_pool")
-        nc.sync.dma_start(ts_pool[TS_ROW:, :], ts[0:1, :])
-        load_q(0, 0, 2)
-        hw_rows = sbuf([P, PACK], F32, PACK * 4, "hw_rows")
-        nc.scalar.dma_start(hw_rows[:], hw[0, 0, :].rearrange("(p c) -> p c", c=PACK))
+        nc.scalar.dma_start(ts_pool[TS_ROW:, :], ts[0:1, :])
 
-        late = [(0, 2), (1, 2), (0, 3), (1, 3)]
-        scale_tile = sbuf([P, (len(late) + 1) * PIECE_BYTES], U8, (len(late) + 1) * PIECE_BYTES, "scale_tile")
+        late = [(1, 1), (0, 2), (1, 2), (0, 3), (1, 3)]
+        scale_tile = sbuf([P, (len(late) + 1) * PIECE_BYTES], U8, (len(late) + 2) * PIECE_BYTES, "scale_tile")
         scale_pool = scale_tile[:, :TOKENS]
-        nc.vector.memset(scale_pool.bitcast(I32), 0)
+        nc.gpsimd.memset(scale_pool.bitcast(I32), 0)
         for r in range(4):
             nc.sync.dma_start(
                 scale_tile[r:P:SHIFT, :TOKENS].bitcast(I32),
                 k_scales[:, r:16:4, :].rearrange("o q t -> q o t").bitcast(I32),
             )
-        word_pool = sbuf([P, TOKENS], U32, TOKENS * 4, "word_pool")
-        nc.sync.dma_start(word_pool[:].bitcast(I32), k_words[0].rearrange("p t b -> p (t b)").bitcast(I32))
+        nc.sync.dma_start(word_pool[:, AHEAD:].bitcast(I32), words[:, AHEAD:])
+        hw_rows = sbuf([P, PACK], F32, PACK * 4, "hw_rows")
+        nc.sync.dma_start(hw_rows[:], hw[0, 0, :].rearrange("(p c) -> p c", c=PACK))
+        load_q(0, 0)
         load_q(1, 0)
-        load_q(1, 1)
+        load_q(0, 1)
 
-        nc.vector.memset(ts_pool[:TS_ROW, :].bitcast(I32), 0)
+        for part in range(0, TOKENS, SLOTS):
+            nc.gpsimd.memset(ts_pool[:TS_ROW, part : part + SLOTS].bitcast(I32), 0)
         ones = sbuf([P, P], F32, P * 4, "ones")
         nc.vector.memset(ones[:], 1.0)
         column = sbuf([P, P], F32, P * 4, "column")
@@ -111,10 +115,16 @@ def tile_attend_tok_idxts_topk_kernel(tc, qT, k_words, k_scales, ts, hw, offs, o
         def cast(o, c, target, copy=nc.scalar.copy):
             copy(target.rearrange("p (g i) t -> p g t i", i=4), raw[o, c].rearrange("p t (g i) -> p g t i", i=4))
 
-        def cast_pass(o, c, copy=nc.scalar.copy):
-            grouped = sbuf([P, QC, PACK], BF16, QC * PACK * 2, f"grouped{o}_{c}")
+        def cast_pass(o, c, copy=nc.scalar.copy, at=None):
+            grouped = sbuf([P, QC, PACK], BF16, QC * PACK * 2, f"grouped{o}_{c}", at)
             cast(o, c, grouped[:], copy)
             return grouped[:].rearrange("p q t -> p (q t)")
+
+        def cast_chunk(c):
+            grouped = sbuf([P, PASSES, QC, PACK], BF16, PASSES * QC * PACK * 2, f"grouped{c}")
+            for o in range(PASSES):
+                cast(o, c, grouped[:, o, :, :])
+            return grouped[:].rearrange("p o q t -> p (o q t)")
 
         def quantise(source, passes, at=None):
             width = len(passes) * QC
@@ -125,57 +135,31 @@ def tile_attend_tok_idxts_topk_kernel(tc, qT, k_words, k_scales, ts, hw, offs, o
             for n, piece in enumerate(passes):
                 codes[piece] = (q_codes[:, n * QC : (n + 1) * QC], q_scale[:, n * QC : (n + 1) * QC])
 
-        hw_wide = sbuf([P, PACK, P], F32, PACK * P * 4, "hw_wide")
-        nc.scalar.copy(hw_wide[:], hw_rows[:].unsqueeze(2).to_broadcast([P, PACK, P]))
-        hw_turned = psum.tile([P, PACK, P], F32, name="hw_turned")
-        for c in range(PACK):
-            nc.tensor.transpose(hw_turned[:, c, :], hw_wide[:, c, :], identity[:])
-        hw_spread = hw_turned[:].rearrange("m c p -> m p c")
-
         ts_listed = sbuf([P, SLOTS], F32, SLOTS * 4, "ts_listed")
         nc.scalar.activation(ts_listed[:], ts_pool[:].indirect(offsets[:]), COPY)
-        quantise(cast_pass(0, 0, nc.vector.tensor_copy), [(0, 0)], place["scale_tile"])
-        ahead = cast_pass(0, 1, nc.vector.tensor_copy)
-        early = LAST * QC
-        hw_early = sbuf([P, early], F32, early * 4, "hw_early", place["ts_pool"])
-        nc.scalar.copy(hw_early[:].rearrange("m (p c) -> m p c", c=PACK), hw_spread[:, : early // PACK, :])
-
         ts_turned = psum.tile([P, KB, P], F32, name="ts_turned")
         for b in range(KB):
             nc.tensor.transpose(ts_turned[:, b, :], ts_listed[:, b * P : (b + 1) * P], identity[:])
         ts_cols = sbuf([P, KB], F32, KB * 4, "ts_cols")
         nc.scalar.copy(ts_cols[:], ts_turned[:, :, TS_ROW])
-        hw_ts = sbuf([P, KB, QC], F32, KB * QC * 4, "hw_ts")
-        for b in range(KB):
-            nc.scalar.activation(
-                hw_ts[:, b, :].rearrange("m (p c) -> m p c", c=PACK),
-                hw_spread[:, early // PACK :, :],
-                COPY,
-                scale=ts_cols[:, b : b + 1],
-            )
+        hw_turned = psum.tile([P, PACK, P], F32, name="hw_turned")
+        for c in range(PACK):
+            nc.tensor.transpose(hw_turned[:, c, :], hw_rows[:, c : c + 1].to_broadcast([P, P]), identity[:])
 
         def factors(blocks, c):
             if c == LAST:
                 return hw_ts[:, blocks.start : blocks.stop, :]
-            return hw_early[:, c * QC : (c + 1) * QC].unsqueeze(1).to_broadcast([P, len(blocks), QC])
+            return hw_all[:, c * QC : (c + 1) * QC].unsqueeze(1).to_broadcast([P, len(blocks), QC])
 
-        word_pairs = []
-        for h in range(2):
-            word_pairs.append(sbuf([P, HALF], U32, HALF * 4, f"word_pairs{h}"))
-            listed = offsets[:, h * HALF // 16 : (h + 1) * HALF // 16]
-            nc.vector.tensor_copy(word_pairs[h][:], word_pool[:].indirect(listed))
-        k_codes = []
-
-        def split(h):
-            k_codes.append(sbuf([P, PASSES, HALF], U16, PASSES * HALF * 2, f"k_codes{h}"))
-            nc.vector.tensor_copy(
-                k_codes[h][:], word_pairs[h][:].bitcast(U16).rearrange("p (i o) -> p o i", o=PASSES)
-            )
+        word_pairs = sbuf([P, SLOTS], U32, SLOTS * 4, "word_pairs")
+        nc.vector.tensor_copy(word_pairs[:], word_pool[:].indirect(offsets[:]))
+        k_codes = sbuf([P, PASSES, SLOTS], U16, PASSES * SLOTS * 2, "k_codes")
+        nc.vector.tensor_copy(k_codes[:], word_pairs[:].bitcast(U16).rearrange("p (i o) -> p o i", o=PASSES))
 
         def multiply(bank, b, o, c, start, stop):
             nc.tensor.matmul_mx(
                 out=bank,
-                lhsT=k_codes[b // 2][:, o, (b % 2) * P : (b % 2 + 1) * P].bitcast(FP4X4),
+                lhsT=k_codes[:, o, b * P : (b + 1) * P].bitcast(FP4X4),
                 lhsT_scale=k_scale[o][:, b * P : (b + 1) * P],
                 rhs=codes[o, c][0].bitcast(FP8X4),
                 rhs_scale=codes[o, c][1],
@@ -186,6 +170,11 @@ def tile_attend_tok_idxts_topk_kernel(tc, qT, k_words, k_scales, ts, hw, offs, o
         def one_pass(bank, blocks, o, c):
             for n, b in enumerate(blocks):
                 multiply(bank[:, n, :], b, o, c, o == 0 and n == 0, o == PASSES - 1 and n == len(blocks) - 1)
+
+        def score(bank, blocks, c):
+            for n, b in enumerate(blocks):
+                for o in range(PASSES):
+                    multiply(bank[:, n, :], b, o, c, o == 0, o == PASSES - 1)
 
         def weigh(target, bank, blocks, c):
             nc.vector.scalar_tensor_tensor(
@@ -204,6 +193,10 @@ def tile_attend_tok_idxts_topk_kernel(tc, qT, k_words, k_scales, ts, hw, offs, o
             nc.gpsimd.tensor_tensor(flat, neighbours[:, :, 0], neighbours[:, :, 1], ALU.add)
             return pairs
 
+        def times_ts(target, source, width):
+            factor = ts_cols[:].unsqueeze(2).to_broadcast([P, KB, width])
+            nc.gpsimd.tensor_tensor(target, source, factor, ALU.mult)
+
         def add_heads(target, source, blocks, c):
             nc.vector.tensor_reduce(
                 out=target[:, blocks.start : blocks.stop, c * RUNS : (c + 1) * RUNS],
@@ -220,45 +213,45 @@ def tile_attend_tok_idxts_topk_kernel(tc, qT, k_words, k_scales, ts, hw, offs, o
         first_banks = [psum.tile([P, 2, QC], F32, name=f"first_bank{h}") for h in range(2)]
         banks = {c: psum.tile([P, KB, QC], F32, name=f"bank{c}") for c in (1, 2)}
         last_banks = [psum.tile([P, 2, QC], F32, name=f"last_bank{h}") for h in range(2)]
+        quantise(cast_chunk(0), [(0, 0), (1, 0)], place["word_pool"])
         for h in range(2):
-            split(h)
-            one_pass(first_banks[h], halves[h], 0, 0)
-        quantise(cast_pass(1, 0), [(1, 0)], place["word_pool"])
-        for h in range(2):
-            one_pass(first_banks[h], halves[h], 1, 0)
-        quantise(ahead, [(0, 1)], place["raw1_0"])
-        one_pass(banks[1], whole, 0, 1)
-        quantise(cast_pass(1, 1), [(1, 1)], place["word_pool"] + PIECE_BYTES)
-        one_pass(banks[1], whole, 1, 1)
-        weighted0 = weigh_into(0, None)
+            score(first_banks[h], halves[h], 0)
+        hw_all = sbuf([P, NQ], F32, NQ * 4, "hw_all", place["raw1_0"])
+        nc.vector.tensor_copy(
+            hw_all[:].rearrange("m (p c) -> m p c", c=PACK), hw_turned[:].rearrange("m c p -> m p c")
+        )
+        for o in range(PASSES):
+            quantise(cast_pass(o, 1), [(o, 1)])
+            one_pass(banks[1], whole, o, 1)
+        weighted0 = weigh_into(0, place["raw1_1"])
         for h in range(2):
             weigh(weighted0, first_banks[h], halves[h], 0)
-        quantise(cast_pass(0, 2), [(0, 2)], place["q_codes1_0"])
+        quantise(cast_pass(0, 2), [(0, 2)], place["q_codes0_0"])
         one_pass(banks[2], whole, 0, 2)
-        pairs0 = pair_heads(0, weighted0[:], place["grouped0_2"])
-        weighted1 = weigh_into(1, place["raw0_2"])
-        weigh(weighted1, banks[1], whole, 1)
+        summed0 = sbuf([P, KB, RUNS], F32, KB * RUNS * 4, "summed0")
+        add_heads(summed0, weighted0, whole, 0)
         quantise(cast_pass(1, 2), [(1, 2)], place["q_codes1_1"])
         one_pass(banks[2], whole, 1, 2)
-        summed = sbuf([P, KB, LAST * RUNS], F32, KB * LAST * RUNS * 4, "summed", place["raw1_2"])
-        add_heads(summed, pairs0, whole, 0)
-        add_heads(summed, weighted1, whole, 1)
-        quantise(cast_pass(0, LAST), [(0, LAST)], place["pairs0"])
+        result = sbuf([P, KB, NQ // HEADS], F32, KB * NQ // HEADS * 4, "result", place["grouped1_2"])
+        times_ts(result[:, :, :RUNS], summed0[:], RUNS)
+        weighted1 = weigh_into(1, place["raw1_2"])
+        weigh(weighted1, banks[1], whole, 1)
+        quantise(cast_pass(0, LAST), [(0, LAST)])
         for h in range(2):
             one_pass(last_banks[h], halves[h], 0, LAST)
+        pairs1 = pair_heads(1, weighted1[:], place["grouped0_3"])
         weighted2 = weigh_into(2, place["raw0_3"])
         weigh(weighted2, banks[2], whole, 2)
         quantise(cast_pass(1, LAST), [(1, LAST)], place["q_codes1_2"])
         for h in range(2):
             one_pass(last_banks[h], halves[h], 1, LAST)
-        add_heads(summed, weighted2, whole, 2)
-        result = sbuf([P, KB, NQ // HEADS], F32, KB * NQ // HEADS * 4, "result")
-        nc.gpsimd.tensor_tensor(
-            result[:, :, : LAST * RUNS],
-            summed[:],
-            ts_cols[:].unsqueeze(2).to_broadcast([P, KB, LAST * RUNS]),
-            ALU.mult,
-        )
+        hw_ts = sbuf([P, KB, QC], F32, KB * QC * 4, "hw_ts", place["raw1_3"] + PIECE_BYTES // 2)
+        for b in range(KB):
+            nc.scalar.activation(hw_ts[:, b, :], hw_all[:, LAST * QC :], COPY, scale=ts_cols[:, b : b + 1])
+        summed = sbuf([P, KB, 2 * RUNS], F32, KB * 2 * RUNS * 4, "summed", place["raw1_3"])
+        add_heads(summed, weighted2, whole, 1)
+        add_heads(summed, pairs1, whole, 0)
+        times_ts(result[:, :, RUNS : LAST * RUNS], summed[:], 2 * RUNS)
         weighted3 = weigh_into(LAST, None)
         for h in range(2):
             weigh(weighted3, last_banks[h], halves[h], LAST)

@@ -71,7 +71,7 @@ def tile_attend_tok_idxts_topk_kernel(tc, qT, k_words, k_scales, ts, hw, offs, o
         late = [(1, 1), (0, 2), (1, 2), (0, 3), (1, 3)]
         scale_tile = sbuf([P, (len(late) + 1) * PIECE_BYTES], U8, (len(late) + 2) * PIECE_BYTES, "scale_tile")
         scale_pool = scale_tile[:, :TOKENS]
-        nc.gpsimd.memset(scale_pool.bitcast(I32), 0)
+        nc.vector.memset(scale_pool.bitcast(I32), 0)
         for r in range(4):
             nc.sync.dma_start(
                 scale_tile[r:P:SHIFT, :TOKENS].bitcast(I32),
@@ -84,20 +84,20 @@ def tile_attend_tok_idxts_topk_kernel(tc, qT, k_words, k_scales, ts, hw, offs, o
         load_q(1, 0)
         load_q(0, 1)
 
-        for part in range(0, TOKENS, SLOTS):
-            nc.gpsimd.memset(ts_pool[:TS_ROW, part : part + SLOTS].bitcast(I32), 0)
         ones = sbuf([P, P], F32, P * 4, "ones")
         nc.vector.memset(ones[:], 1.0)
         column = sbuf([P, P], F32, P * 4, "column")
         nc.vector.tensor_tensor_scan(column[:], ones[:], ones[:], 0.0, ALU.mult, ALU.add)
         turned = sbuf([P, P], F32, P * 4, "turned")
         nc.vector.transpose(turned[:], column[:])
-        identity = sbuf([P, P], F32, P * 4, "identity")
+        row = sbuf([P, 1], F32, 4, "row")
         for first in range(0, P, QUADRANT):
             rows = slice(first, first + QUADRANT)
-            nc.vector.tensor_scalar(
-                identity[rows, :], column[rows, :], turned[rows, first : first + 1], None, ALU.is_equal
-            )
+            nc.scalar.copy(row[rows, :], turned[rows, first : first + 1])
+        for part in range(0, TOKENS, SLOTS):
+            nc.vector.memset(ts_pool[:TS_ROW, part : part + SLOTS].bitcast(I32), 0)
+        identity = sbuf([P, P], F32, P * 4, "identity")
+        nc.vector.tensor_scalar(identity[:], column[:], row[:], None, ALU.is_equal)
 
         k_scale = [sbuf([P, SLOTS], U8, SLOTS, f"k_scale{o}") for o in range(PASSES)]
         nc.vector.memset(k_scale[1][:].bitcast(I32), 0)

@@ -51,7 +51,6 @@ def tile_attend_tok_idxts_topk_kernel(tc, qT, k_words, k_scales, ts, hw, offs, o
             return main.tile(shape, dtype, name=name, align_bytes=ALIGN, offset=at)
 
         offsets = keep.tile([P, SLOTS // 16], U16, name="offsets")
-        nc.sync.dma_start(offsets[:], offs)
 
         raw = {}
 
@@ -65,10 +64,11 @@ def tile_attend_tok_idxts_topk_kernel(tc, qT, k_words, k_scales, ts, hw, offs, o
         word_pool = sbuf([P, TOKENS], U32, TOKENS * 4, "word_pool")
         words = k_words[0].rearrange("p t b -> p (t b)").bitcast(I32)
         nc.sync.dma_start(word_pool[:, :AHEAD].bitcast(I32), words[:, :AHEAD])
+        nc.sync.dma_start(offsets[:], offs)
         ts_pool = sbuf([P, TOKENS], F32, TOKENS * 4, "ts_pool")
         nc.scalar.dma_start(ts_pool[TS_ROW:, :], ts[0:1, :])
 
-        late = [(1, 1), (0, 2), (1, 2), (0, 3), (1, 3)]
+        late = [(1, 1), (1, 2), (0, 3), (1, 3)]
         scale_tile = sbuf([P, (len(late) + 1) * PIECE_BYTES], U8, (len(late) + 2) * PIECE_BYTES, "scale_tile")
         scale_pool = scale_tile[:, :TOKENS]
         nc.vector.memset(scale_pool.bitcast(I32), 0)
@@ -82,7 +82,7 @@ def tile_attend_tok_idxts_topk_kernel(tc, qT, k_words, k_scales, ts, hw, offs, o
         nc.sync.dma_start(hw_rows[:], hw[0, 0, :].rearrange("(p c) -> p c", c=PACK))
         load_q(0, 0)
         load_q(1, 0)
-        load_q(0, 1)
+        load_q(0, 1, 2)
 
         ones = sbuf([P, P], F32, P * 4, "ones")
         nc.vector.memset(ones[:], 1.0)
@@ -151,15 +151,23 @@ def tile_attend_tok_idxts_topk_kernel(tc, qT, k_words, k_scales, ts, hw, offs, o
                 return hw_ts[:, blocks.start : blocks.stop, :]
             return hw_all[:, c * QC : (c + 1) * QC].unsqueeze(1).to_broadcast([P, len(blocks), QC])
 
-        word_pairs = sbuf([P, SLOTS], U32, SLOTS * 4, "word_pairs")
-        nc.vector.tensor_copy(word_pairs[:], word_pool[:].indirect(offsets[:]))
-        k_codes = sbuf([P, PASSES, SLOTS], U16, PASSES * SLOTS * 2, "k_codes")
-        nc.vector.tensor_copy(k_codes[:], word_pairs[:].bitcast(U16).rearrange("p (i o) -> p o i", o=PASSES))
+        word_pairs = []
+        for h in range(2):
+            word_pairs.append(sbuf([P, HALF], U32, HALF * 4, f"word_pairs{h}"))
+            listed = offsets[:, h * HALF // 16 : (h + 1) * HALF // 16]
+            nc.vector.tensor_copy(word_pairs[h][:], word_pool[:].indirect(listed))
+        k_codes = []
+
+        def split(h):
+            k_codes.append(sbuf([P, PASSES, HALF], U16, PASSES * HALF * 2, f"k_codes{h}"))
+            nc.vector.tensor_copy(
+                k_codes[h][:], word_pairs[h][:].bitcast(U16).rearrange("p (i o) -> p o i", o=PASSES)
+            )
 
         def multiply(bank, b, o, c, start, stop):
             nc.tensor.matmul_mx(
                 out=bank,
-                lhsT=k_codes[:, o, b * P : (b + 1) * P].bitcast(FP4X4),
+                lhsT=k_codes[b // 2][:, o, (b % 2) * P : (b % 2 + 1) * P].bitcast(FP4X4),
                 lhsT_scale=k_scale[o][:, b * P : (b + 1) * P],
                 rhs=codes[o, c][0].bitcast(FP8X4),
                 rhs_scale=codes[o, c][1],
@@ -213,24 +221,31 @@ def tile_attend_tok_idxts_topk_kernel(tc, qT, k_words, k_scales, ts, hw, offs, o
         first_banks = [psum.tile([P, 2, QC], F32, name=f"first_bank{h}") for h in range(2)]
         banks = {c: psum.tile([P, KB, QC], F32, name=f"bank{c}") for c in (1, 2)}
         last_banks = [psum.tile([P, 2, QC], F32, name=f"last_bank{h}") for h in range(2)]
-        quantise(cast_chunk(0), [(0, 0), (1, 0)], place["word_pool"])
+        split(0)
+        quantise(cast_pass(0, 0), [(0, 0)], place["word_pool"] + PIECE_BYTES)
+        one_pass(first_banks[0], halves[0], 0, 0)
+        split(1)
+        one_pass(first_banks[1], halves[1], 0, 0)
+        quantise(cast_pass(1, 0), [(1, 0)], place["word_pool"])
         for h in range(2):
-            score(first_banks[h], halves[h], 0)
+            one_pass(first_banks[h], halves[h], 1, 0)
         hw_all = sbuf([P, NQ], F32, NQ * 4, "hw_all", place["raw1_0"])
-        nc.vector.tensor_copy(
-            hw_all[:].rearrange("m (p c) -> m p c", c=PACK), hw_turned[:].rearrange("m c p -> m p c")
-        )
-        for o in range(PASSES):
-            quantise(cast_pass(o, 1), [(o, 1)])
-            one_pass(banks[1], whole, o, 1)
-        weighted0 = weigh_into(0, place["raw1_1"])
-        for h in range(2):
-            weigh(weighted0, first_banks[h], halves[h], 0)
-        quantise(cast_pass(0, 2), [(0, 2)], place["q_codes0_0"])
+        nc.scalar.copy(hw_all[:].rearrange("m (p c) -> m p c", c=PACK), hw_turned[:].rearrange("m c p -> m p c"))
+        ahead = cast_pass(0, 2, nc.vector.tensor_copy, place["word_pairs1"])
+        front = range(KB // 2)
+        first_weighted = [sbuf([P, KB // 2, QC], F32, KB * QC * 2, f"first_weighted{h}") for h in range(2)]
+        weigh(first_weighted[0], first_banks[0], front, 0)
+        quantise(cast_pass(0, 1), [(0, 1)], place["q_codes1_0"])
+        one_pass(banks[1], whole, 0, 1)
+        weigh(first_weighted[1], first_banks[1], front, 0)
+        quantise(ahead, [(0, 2)], place["q_codes0_0"])
+        quantise(cast_pass(1, 1), [(1, 1)])
+        one_pass(banks[1], whole, 1, 1)
         one_pass(banks[2], whole, 0, 2)
-        summed0 = sbuf([P, KB, RUNS], F32, KB * RUNS * 4, "summed0")
-        add_heads(summed0, weighted0, whole, 0)
-        quantise(cast_pass(1, 2), [(1, 2)], place["q_codes1_1"])
+        summed0 = sbuf([P, KB, RUNS], F32, KB * RUNS * 4, "summed0", place["raw1_1"])
+        for h, blocks in enumerate(halves):
+            add_heads(summed0[:, blocks.start : blocks.stop, :], first_weighted[h], front, 0)
+        quantise(cast_pass(1, 2), [(1, 2)], place["first_weighted0"])
         one_pass(banks[2], whole, 1, 2)
         result = sbuf([P, KB, NQ // HEADS], F32, KB * NQ // HEADS * 4, "result", place["grouped1_2"])
         times_ts(result[:, :, :RUNS], summed0[:], RUNS)

@@ -68,8 +68,8 @@ def tile_attend_tok_idxts_topk_kernel(tc, qT, k_words, k_scales, ts, hw, offs, o
         ts_pool = sbuf([P, TOKENS], F32, TOKENS * 4, "ts_pool")
         nc.scalar.dma_start(ts_pool[TS_ROW:, :], ts[0:1, :])
 
-        late = [(1, 1), (1, 2), (0, 3), (1, 3)]
-        scale_tile = sbuf([P, (len(late) + 1) * PIECE_BYTES], U8, (len(late) + 2) * PIECE_BYTES, "scale_tile")
+        late = [(0, 1, 2), (1, 1, 1), (1, 2, 1), (0, 3, 1), (1, 3, 1)]
+        scale_tile = sbuf([P, (len(late) + 2) * PIECE_BYTES], U8, (len(late) + 3) * PIECE_BYTES, "scale_tile")
         scale_pool = scale_tile[:, :TOKENS]
         nc.vector.memset(scale_pool.bitcast(I32), 0)
         for r in range(4):
@@ -82,7 +82,6 @@ def tile_attend_tok_idxts_topk_kernel(tc, qT, k_words, k_scales, ts, hw, offs, o
         nc.sync.dma_start(hw_rows[:], hw[0, 0, :].rearrange("(p c) -> p c", c=PACK))
         load_q(0, 0)
         load_q(1, 0)
-        load_q(0, 1, 2)
 
         ones = sbuf([P, P], F32, P * 4, "ones")
         nc.vector.memset(ones[:], 1.0)
@@ -107,8 +106,10 @@ def tile_attend_tok_idxts_topk_kernel(tc, qT, k_words, k_scales, ts, hw, offs, o
                 k_scale[1][first : first + rows, :].bitcast(I32),
                 k_scale[0][first + SHIFT : first + SHIFT + rows, :].bitcast(I32),
             )
-        for n, (o, c) in enumerate(late):
-            load_q(o, c, 1, place["scale_tile"] + (n + 1) * PIECE_BYTES)
+        at = place["scale_tile"] + PIECE_BYTES
+        for o, c, chunks in late:
+            load_q(o, c, chunks, at)
+            at = at + chunks * PIECE_BYTES
 
         codes = {}
 

@@ -28,7 +28,8 @@ SHIFT = 16
 TS_ROW = P - 1
 QUADRANT = 32
 HALF = SLOTS // 2
-AHEAD = TOKENS // 4
+SHARE = 160
+AHEAD = TOKENS // 8
 ALIGN = 256
 PIECE_BYTES = PACK * QC * 4
 
@@ -58,8 +59,7 @@ def tile_attend_tok_idxts_topk_kernel(tc, qT, k_words, k_scales, ts, hw, offs, o
             piece = sbuf([P, PACK, chunks * QC], F32, chunks * PIECE_BYTES, f"raw{o}_{c}", at)
             rows = qT[0, o * K_PASS : (o + 1) * K_PASS, c * QC : (c + chunks) * QC]
             nc.sync.dma_start(piece[:], rows.rearrange("(p t) q -> p t q", t=PACK))
-            for n in range(chunks):
-                raw[o, c + n] = piece[:, :, n * QC : (n + 1) * QC]
+            raw[o, c] = piece[:]
 
         word_pool = sbuf([P, TOKENS], U32, TOKENS * 4, "word_pool")
         words = k_words[0].rearrange("p t b -> p (t b)").bitcast(I32)
@@ -93,8 +93,10 @@ def tile_attend_tok_idxts_topk_kernel(tc, qT, k_words, k_scales, ts, hw, offs, o
         for first in range(0, P, QUADRANT):
             rows = slice(first, first + QUADRANT)
             nc.scalar.copy(row[rows, :], turned[rows, first : first + 1])
-        for part in range(0, TOKENS, SLOTS):
+        for part in range(0, TOKENS // 2, SLOTS):
             nc.vector.memset(ts_pool[:TS_ROW, part : part + SLOTS].bitcast(I32), 0)
+        for part in range(TOKENS // 2, TOKENS, SLOTS):
+            nc.gpsimd.memset(ts_pool[:TS_ROW, part : part + SLOTS].bitcast(I32), 0)
         identity = sbuf([P, P], F32, P * 4, "identity")
         nc.vector.tensor_scalar(identity[:], column[:], row[:], None, ALU.is_equal)
 
@@ -232,14 +234,22 @@ def tile_attend_tok_idxts_topk_kernel(tc, qT, k_words, k_scales, ts, hw, offs, o
             one_pass(first_banks[h], halves[h], 1, 0)
         hw_all = sbuf([P, NQ], F32, NQ * 4, "hw_all", place["raw1_0"])
         nc.scalar.copy(hw_all[:].rearrange("m (p c) -> m p c", c=PACK), hw_turned[:].rearrange("m c p -> m p c"))
-        ahead = cast_pass(0, 2, nc.vector.tensor_copy, place["word_pairs1"])
+        wide = raw[0, 1]
+        ahead = sbuf([P, 2 * QC, PACK], BF16, 2 * QC * PACK * 2, "ahead", place["word_pairs0"])
+        for columns, copy in ((slice(0, SHARE), nc.vector.tensor_copy), (slice(SHARE, 2 * QC), nc.scalar.copy)):
+            copy(
+                ahead[:, columns, :].rearrange("p (g i) t -> p g t i", i=4),
+                wide[:, :, columns].rearrange("p t (g i) -> p g t i", i=4),
+            )
         front = range(KB // 2)
-        first_weighted = [sbuf([P, KB // 2, QC], F32, KB * QC * 2, f"first_weighted{h}") for h in range(2)]
+        first_weighted = [
+            sbuf([P, KB // 2, QC], F32, KB * QC * 2, f"first_weighted{h}", place["raw0_1"] + h * KB * QC * 2)
+            for h in range(2)
+        ]
         weigh(first_weighted[0], first_banks[0], front, 0)
-        quantise(cast_pass(0, 1), [(0, 1)], place["q_codes1_0"])
+        quantise(ahead[:].rearrange("p q t -> p (q t)"), [(0, 1), (0, 2)])
         one_pass(banks[1], whole, 0, 1)
         weigh(first_weighted[1], first_banks[1], front, 0)
-        quantise(ahead, [(0, 2)], place["q_codes0_0"])
         quantise(cast_pass(1, 1), [(1, 1)])
         one_pass(banks[1], whole, 1, 1)
         one_pass(banks[2], whole, 0, 2)

@@ -93,10 +93,8 @@ def tile_attend_tok_idxts_topk_kernel(tc, qT, k_words, k_scales, ts, hw, offs, o
         for first in range(0, P, QUADRANT):
             rows = slice(first, first + QUADRANT)
             nc.scalar.copy(row[rows, :], turned[rows, first : first + 1])
-        for part in range(0, TOKENS // 2, SLOTS):
+        for part in range(0, TOKENS, SLOTS):
             nc.vector.memset(ts_pool[:TS_ROW, part : part + SLOTS].bitcast(I32), 0)
-        for part in range(TOKENS // 2, TOKENS, SLOTS):
-            nc.gpsimd.memset(ts_pool[:TS_ROW, part : part + SLOTS].bitcast(I32), 0)
         identity = sbuf([P, P], F32, P * 4, "identity")
         nc.vector.tensor_scalar(identity[:], column[:], row[:], None, ALU.is_equal)
 

@@ -245,11 +245,12 @@ def tile_attend_tok_idxts_topk_kernel(tc, qT, k_words, k_scales, ts, hw, offs, o
             for h in range(2)
         ]
         weigh(first_weighted[0], first_banks[0], front, 0)
-        quantise(ahead[:].rearrange("p q t -> p (q t)"), [(0, 1), (0, 2)])
+        quantise(ahead[:, :QC, :].rearrange("p q t -> p (q t)"), [(0, 1)])
         one_pass(banks[1], whole, 0, 1)
         weigh(first_weighted[1], first_banks[1], front, 0)
         quantise(cast_pass(1, 1), [(1, 1)])
         one_pass(banks[1], whole, 1, 1)
+        quantise(ahead[:, QC:, :].rearrange("p q t -> p (q t)"), [(0, 2)], place["raw1_1"] + PIECE_BYTES // 2)
         one_pass(banks[2], whole, 0, 2)
         summed0 = sbuf([P, KB, RUNS], F32, KB * RUNS * 4, "summed0", place["raw1_1"])
         for h, blocks in enumerate(halves):

@@ -99,7 +99,7 @@ def tile_attend_tok_idxts_topk_kernel(tc, qT, k_words, k_scales, ts, hw, offs, o
         nc.vector.tensor_scalar(identity[:], column[:], row[:], None, ALU.is_equal)
 
         k_scale = [sbuf([P, SLOTS], U8, SLOTS, f"k_scale{o}") for o in range(PASSES)]
-        nc.vector.memset(k_scale[1][:].bitcast(I32), 0)
+        nc.vector.memset(k_scale[1][P // 2 :, :].bitcast(I32), 0)
         nc.vector.tensor_copy(k_scale[0][:], scale_pool.indirect(offsets[:]))
         for first, rows in ((0, 64), (64, 4), (96, 4)):
             nc.sync.dma_start(

from contextlib import ExitStack

import concourse.mybir as mybir

F32 = mybir.dt.float32
BF16 = mybir.dt.bfloat16
I32 = mybir.dt.int32
U32 = mybir.dt.uint32
U16 = mybir.dt.uint16
U8 = mybir.dt.uint8
FP8X4 = mybir.dt.float8_e4m3fn_x4
FP4X4 = mybir.dt.float4_e2m1fn_x4
ALU = mybir.AluOpType
AX = mybir.AxisListType
COPY = mybir.ActivationFunctionType.Copy

P = 128
PACK = 4
PASSES = 2
K_PASS = P * PACK
SLOTS, TOKENS, D, NQ, HEADS = 512, 2048, 1024, 512, 16
QC = 128
CHUNKS = NQ // QC
LAST = CHUNKS - 1
KB = SLOTS // P
RUNS = QC // HEADS
SHIFT = 16
TS_ROW = P - 1
QUADRANT = 32
HALF = SLOTS // 2
SHARE = 160
AHEAD = TOKENS // 8
ALIGN = 256
PIECE_BYTES = PACK * QC * 4

FLOPS = 2 * SLOTS * D * NQ


def tile_attend_tok_idxts_topk_kernel(tc, qT, k_words, k_scales, ts, hw, offs, out):
    nc = tc.nc
    with ExitStack() as ctx:
        keep = ctx.enter_context(tc.tile_pool(name="keep", bufs=1))
        main = ctx.enter_context(tc.tile_pool(name="main", bufs=1))
        psum = ctx.enter_context(tc.psum_pool(name="psum", bufs=1))
        place = {"free": 0}

        def sbuf(shape, dtype, size, name, at=None):
            if at is None:
                at = place["free"]
                place["free"] = at + (size + ALIGN - 1) // ALIGN * ALIGN
            place[name] = at
            return main.tile(shape, dtype, name=name, align_bytes=ALIGN, offset=at)

        offsets = keep.tile([P, SLOTS // 16], U16, name="offsets")

        raw = {}

        def load_q(o, c, chunks=1, at=None):
            piece = sbuf([P, PACK, chunks * QC], F32, chunks * PIECE_BYTES, f"raw{o}_{c}", at)
            rows = qT[0, o * K_PASS : (o + 1) * K_PASS, c * QC : (c + chunks) * QC]
            nc.sync.dma_start(piece[:], rows.rearrange("(p t) q -> p t q", t=PACK))
            raw[o, c] = piece[:]

        word_pool = sbuf([P, TOKENS], U32, TOKENS * 4, "word_pool")
        words = k_words[0].rearrange("p t b -> p (t b)").bitcast(I32)
        nc.sync.dma_start(word_pool[:, :AHEAD].bitcast(I32), words[:, :AHEAD])
        nc.sync.dma_start(offsets[:], offs)
        ts_pool = sbuf([P, TOKENS], F32, TOKENS * 4, "ts_pool")
        nc.scalar.dma_start(ts_pool[TS_ROW:, :], ts[0:1, :])

        late = [(0, 1, 2), (1, 1, 1), (1, 2, 1), (0, 3, 1), (1, 3, 1)]
        scale_tile = sbuf([P, (len(late) + 2) * PIECE_BYTES], U8, (len(late) + 3) * PIECE_BYTES, "scale_tile")
        scale_pool = scale_tile[:, :TOKENS]
        nc.vector.memset(scale_pool.bitcast(I32), 0)
        for r in range(4):
            nc.sync.dma_start(
                scale_tile[r:P:SHIFT, :TOKENS].bitcast(I32),
                k_scales[:, r:16:4, :].rearrange("o q t -> q o t").bitcast(I32),
            )
        nc.sync.dma_start(word_pool[:, AHEAD:].bitcast(I32), words[:, AHEAD:])
        hw_rows = sbuf([P, PACK], F32, PACK * 4, "hw_rows")
        nc.sync.dma_start(hw_rows[:], hw[0, 0, :].rearrange("(p c) -> p c", c=PACK))
        load_q(0, 0)
        load_q(1, 0)

        ones = sbuf([P, P], F32, P * 4, "ones")
        nc.vector.memset(ones[:], 1.0)
        column = sbuf([P, P], F32, P * 4, "column")
        nc.vector.tensor_tensor_scan(column[:], ones[:], ones[:], 0.0, ALU.mult, ALU.add)
        turned = sbuf([P, P], F32, P * 4, "turned")
        nc.vector.transpose(turned[:], column[:])
        row = sbuf([P, 1], F32, 4, "row")
        for first in range(0, P, QUADRANT):
            rows = slice(first, first + QUADRANT)
            nc.scalar.copy(row[rows, :], turned[rows, first : first + 1])
        for part in range(0, TOKENS, SLOTS):
            nc.vector.memset(ts_pool[:TS_ROW, part : part + SLOTS].bitcast(I32), 0)
        identity = sbuf([P, P], F32, P * 4, "identity")
        nc.vector.tensor_scalar(identity[:], column[:], row[:], None, ALU.is_equal)

        k_scale = [sbuf([P, SLOTS], U8, SLOTS, f"k_scale{o}") for o in range(PASSES)]
        nc.vector.memset(k_scale[1][P // 2 :, :].bitcast(I32), 0)
        nc.vector.tensor_copy(k_scale[0][:], scale_pool.indirect(offsets[:]))
        for first, rows in ((0, 64), (64, 4), (96, 4)):
            nc.sync.dma_start(
                k_scale[1][first : first + rows, :].bitcast(I32),
                k_scale[0][first + SHIFT : first + SHIFT + rows, :].bitcast(I32),
            )
        at = place["scale_tile"] + PIECE_BYTES
        for o, c, chunks in late:
            load_q(o, c, chunks, at)
            at = at + chunks * PIECE_BYTES

        codes = {}

        def cast(o, c, target, copy=nc.scalar.copy):
            copy(target.rearrange("p (g i) t -> p g t i", i=4), raw[o, c].rearrange("p t (g i) -> p g t i", i=4))

        def cast_pass(o, c, copy=nc.scalar.copy, at=None):
            grouped = sbuf([P, QC, PACK], BF16, QC * PACK * 2, f"grouped{o}_{c}", at)
            cast(o, c, grouped[:], copy)
            return grouped[:].rearrange("p q t -> p (q t)")

        def cast_chunk(c):
            grouped = sbuf([P, PASSES, QC, PACK], BF16, PASSES * QC * PACK * 2, f"grouped{c}")
            for o in range(PASSES):
                cast(o, c, grouped[:, o, :, :])
            return grouped[:].rearrange("p o q t -> p (o q t)")

        def quantise(source, passes, at=None):
            width = len(passes) * QC
            name = f"{passes[0][0]}_{passes[0][1]}"
            q_codes = sbuf([P, width], U32, width * 4, f"q_codes{name}", at)
            q_scale = sbuf([P, width], U8, width, f"q_scale{name}")
            nc.vector.quantize_mx(out=q_codes[:].bitcast(FP8X4), scales=q_scale[:], in_=source)
            for n, piece in enumerate(passes):
                codes[piece] = (q_codes[:, n * QC : (n + 1) * QC], q_scale[:, n * QC : (n + 1) * QC])

        ts_listed = sbuf([P, SLOTS], F32, SLOTS * 4, "ts_listed")
        nc.scalar.activation(ts_listed[:], ts_pool[:].indirect(offsets[:]), COPY)
        ts_turned = psum.tile([P, KB, P], F32, name="ts_turned")
        for b in range(KB):
            nc.tensor.transpose(ts_turned[:, b, :], ts_listed[:, b * P : (b + 1) * P], identity[:])
        ts_cols = sbuf([P, KB], F32, KB * 4, "ts_cols")
        nc.scalar.copy(ts_cols[:], ts_turned[:, :, TS_ROW])
        hw_turned = psum.tile([P, PACK, P], F32, name="hw_turned")
        for c in range(PACK):
            nc.tensor.transpose(hw_turned[:, c, :], hw_rows[:, c : c + 1].to_broadcast([P, P]), identity[:])

        def factors(blocks, c):
            if c == LAST:
                return hw_ts[:, blocks.start : blocks.stop, :]
            return hw_all[:, c * QC : (c + 1) * QC].unsqueeze(1).to_broadcast([P, len(blocks), QC])

        word_pairs = []
        for h in range(2):
            word_pairs.append(sbuf([P, HALF], U32, HALF * 4, f"word_pairs{h}"))
            listed = offsets[:, h * HALF // 16 : (h + 1) * HALF // 16]
            nc.vector.tensor_copy(word_pairs[h][:], word_pool[:].indirect(listed))
        k_codes = []

        def split(h):
            k_codes.append(sbuf([P, PASSES, HALF], U16, PASSES * HALF * 2, f"k_codes{h}"))
            nc.vector.tensor_copy(
                k_codes[h][:], word_pairs[h][:].bitcast(U16).rearrange("p (i o) -> p o i", o=PASSES)
            )

        def multiply(bank, b, o, c, start, stop):
            nc.tensor.matmul_mx(
                out=bank,
                lhsT=k_codes[b // 2][:, o, (b % 2) * P : (b % 2 + 1) * P].bitcast(FP4X4),
                lhsT_scale=k_scale[o][:, b * P : (b + 1) * P],
                rhs=codes[o, c][0].bitcast(FP8X4),
                rhs_scale=codes[o, c][1],
                start=start,
                stop=stop,
            )

        def one_pass(bank, blocks, o, c):
            for n, b in enumerate(blocks):
                multiply(bank[:, n, :], b, o, c, o == 0 and n == 0, o == PASSES - 1 and n == len(blocks) - 1)

        def score(bank, blocks, c):
            for n, b in enumerate(blocks):
                for o in range(PASSES):
                    multiply(bank[:, n, :], b, o, c, o == 0, o == PASSES - 1)

        def weigh(target, bank, blocks, c):
            nc.vector.scalar_tensor_tensor(
                out=target[:, blocks.start : blocks.stop, :],
                in0=bank[:],
                scalar=0.0,
                in1=factors(blocks, c),
                op0=ALU.max,
                op1=ALU.mult,
            )

        def pair_heads(c, source, at):
            neighbours = source.rearrange("p b (m e) -> p (b m) e", e=2)
            pairs = sbuf([P, KB, QC // 2], F32, KB * QC * 2, f"pairs{c}", at)
            flat = pairs[:].rearrange("p b m -> p (b m)")
            nc.gpsimd.tensor_tensor(flat, neighbours[:, :, 0], neighbours[:, :, 1], ALU.add)
            return pairs

        def times_ts(target, source, width):
            factor = ts_cols[:].unsqueeze(2).to_broadcast([P, KB, width])
            nc.gpsimd.tensor_tensor(target, source, factor, ALU.mult)

        def add_heads(target, source, blocks, c):
            nc.vector.tensor_reduce(
                out=target[:, blocks.start : blocks.stop, c * RUNS : (c + 1) * RUNS],
                in_=source[:, blocks.start : blocks.stop, :].rearrange("p b (j s) -> p b j s", j=RUNS),
                axis=AX.X,
                op=ALU.add,
            )

        def weigh_into(c, at):
            return sbuf([P, KB, QC], F32, KB * QC * 4, f"weighted{c}", at)

        halves = [range(0, KB // 2), range(KB // 2, KB)]
        whole = range(KB)
        first_banks = [psum.tile([P, 2, QC], F32, name=f"first_bank{h}") for h in range(2)]
        banks = {c: psum.tile([P, KB, QC], F32, name=f"bank{c}") for c in (1, 2)}
        last_banks = [psum.tile([P, 2, QC], F32, name=f"last_bank{h}") for h in range(2)]
        split(0)
        quantise(cast_pass(0, 0), [(0, 0)], place["word_pool"] + PIECE_BYTES)
        one_pass(first_banks[0], halves[0], 0, 0)
        split(1)
        one_pass(first_banks[1], halves[1], 0, 0)
        quantise(cast_pass(1, 0), [(1, 0)], place["word_pool"])
        for h in range(2):
            one_pass(first_banks[h], halves[h], 1, 0)
        hw_all = sbuf([P, NQ], F32, NQ * 4, "hw_all", place["raw1_0"])
        nc.scalar.copy(hw_all[:].rearrange("m (p c) -> m p c", c=PACK), hw_turned[:].rearrange("m c p -> m p c"))
        wide = raw[0, 1]
        ahead = sbuf([P, 2 * QC, PACK], BF16, 2 * QC * PACK * 2, "ahead", place["word_pairs0"])
        for columns, copy in ((slice(0, SHARE), nc.vector.tensor_copy), (slice(SHARE, 2 * QC), nc.scalar.copy)):
            copy(
                ahead[:, columns, :].rearrange("p (g i) t -> p g t i", i=4),
                wide[:, :, columns].rearrange("p t (g i) -> p g t i", i=4),
            )
        front = range(KB // 2)
        first_weighted = [
            sbuf([P, KB // 2, QC], F32, KB * QC * 2, f"first_weighted{h}", place["raw0_1"] + h * KB * QC * 2)
            for h in range(2)
        ]
        weigh(first_weighted[0], first_banks[0], front, 0)
        quantise(ahead[:, :QC, :].rearrange("p q t -> p (q t)"), [(0, 1)])
        one_pass(banks[1], whole, 0, 1)
        weigh(first_weighted[1], first_banks[1], front, 0)
        quantise(cast_pass(1, 1), [(1, 1)])
        one_pass(banks[1], whole, 1, 1)
        quantise(ahead[:, QC:, :].rearrange("p q t -> p (q t)"), [(0, 2)], place["raw1_1"] + PIECE_BYTES // 2)
        one_pass(banks[2], whole, 0, 2)
        summed0 = sbuf([P, KB, RUNS], F32, KB * RUNS * 4, "summed0", place["raw1_1"])
        for h, blocks in enumerate(halves):
            add_heads(summed0[:, blocks.start : blocks.stop, :], first_weighted[h], front, 0)
        quantise(cast_pass(1, 2), [(1, 2)], place["first_weighted0"])
        one_pass(banks[2], whole, 1, 2)
        result = sbuf([P, KB, NQ // HEADS], F32, KB * NQ // HEADS * 4, "result", place["grouped1_2"])
        times_ts(result[:, :, :RUNS], summed0[:], RUNS)
        weighted1 = weigh_into(1, place["raw1_2"])
        weigh(weighted1, banks[1], whole, 1)
        quantise(cast_pass(0, LAST), [(0, LAST)])
        for h in range(2):
            one_pass(last_banks[h], halves[h], 0, LAST)
        pairs1 = pair_heads(1, weighted1[:], place["grouped0_3"])
        weighted2 = weigh_into(2, place["raw0_3"])
        weigh(weighted2, banks[2], whole, 2)
        quantise(cast_pass(1, LAST), [(1, LAST)], place["q_codes1_2"])
        for h in range(2):
            one_pass(last_banks[h], halves[h], 1, LAST)
        hw_ts = sbuf([P, KB, QC], F32, KB * QC * 4, "hw_ts", place["raw1_3"] + PIECE_BYTES // 2)
        for b in range(KB):
            nc.scalar.activation(hw_ts[:, b, :], hw_all[:, LAST * QC :], COPY, scale=ts_cols[:, b : b + 1])
        summed = sbuf([P, KB, 2 * RUNS], F32, KB * 2 * RUNS * 4, "summed", place["raw1_3"])
        add_heads(summed, weighted2, whole, 1)
        add_heads(summed, pairs1, whole, 0)
        times_ts(result[:, :, RUNS : LAST * RUNS], summed[:], 2 * RUNS)
        weighted3 = weigh_into(LAST, None)
        for h in range(2):
            weigh(weighted3, last_banks[h], halves[h], LAST)
        rows = out[0].rearrange("(b p) j -> p b j", p=P)
        for blocks in halves:
            add_heads(result, weighted3, blocks, LAST)
            nc.sync.dma_start(rows[:, blocks.start : blocks.stop, :], result[:, blocks.start : blocks.stop, :])
